import numpy as np
import ml_dtypes


def mxq(x, axis, fmt="e4m3"):
    dtype, down = {"e4m3": (ml_dtypes.float8_e4m3fn, 7), "e5m2": (ml_dtypes.float8_e5m2, 14)}[fmt]
    v = np.moveaxis(np.asarray(x, np.float32).astype(ml_dtypes.bfloat16).astype(np.float64), axis, -1)
    blocks = v.reshape(v.shape[:-1] + (-1, 32))
    amax = np.abs(blocks).max(-1, keepdims=True)
    byte = np.maximum(np.where(amax > 0, np.frexp(amax)[1] - 1 + 127, 0) - down, 1)
    scale = np.exp2(byte - 127.0)
    codes = (blocks / scale).astype(np.float32).astype(dtype).astype(np.float64)
    return np.moveaxis((codes * scale).reshape(v.shape), -1, axis)


WIDE = False


def mx_kscale(k):
    if not WIDE:
        return np.ones(k)
    levels = np.array([10, -10, 5, -5, 0])
    if k % 512:
        return np.exp2(np.random.permutation(np.resize(levels, k // 32))).repeat(32)
    a = np.empty((k // 512, 16))
    for p in range(k // 512):
        a[p, :8] = np.random.permutation(np.resize(levels, 8))
        for g in range(8):
            far = levels[np.abs(levels - a[p, g]) >= 10]
            a[p, g + 8] = far[np.random.randint(len(far))]
    return np.exp2(a.ravel()).repeat(32)


def f64(x):
    return np.asarray(x).astype(np.float64)


def striped(idx):
    return np.tile(idx.reshape(-1, 16).T, (8, 1)).astype(np.uint16)


def unstriped(offs):
    return offs[:16].T.reshape(-1).astype(np.int64)


E2M1 = np.array([0.0, 0.5, 1.0, 1.5, 2.0, 3.0, 4.0, 6.0, -0.0, -0.5, -1.0, -1.5, -2.0, -3.0, -4.0, -6.0])


def pack_weight(w, fmt):
    k, n = w.shape
    w = f64(np.asarray(w, np.float32).astype(ml_dtypes.bfloat16)).reshape(k // 32, 32, n)
    amax = np.abs(w).max(1)
    if fmt == "e4m3":
        byte = np.frexp(amax)[1] - 1 + 127 - 7
    else:
        mant, ex = np.frexp(amax / 6.0)
        byte = np.where(mant > 0.5, ex, ex - 1) + 127
    byte = np.clip(np.where(amax > 0, byte, 1), 1, 254)
    scaled = (w * np.exp2(127.0 - byte)[:, None, :]).reshape(k, n).astype(np.float32)
    by_word = np.ascontiguousarray(scaled.reshape(k // 512, 128, 4, n).transpose(0, 1, 3, 2))
    if fmt == "e4m3":
        words = by_word.astype(ml_dtypes.float8_e4m3fn).view(np.uint8)
    else:
        c = by_word.astype(ml_dtypes.float4_e2m1fn).view(np.uint8) & 0xF
        words = (c[..., 0::2] | (c[..., 1::2] << 4)).reshape(k // 512, 128, 2 * n)
    return np.ascontiguousarray(words), np.ascontiguousarray(byte.astype(np.uint8).reshape(k // 512, 16, n))


def unpack_weight(words, scales, fmt):
    g, _, n = scales.shape
    words = np.ascontiguousarray(words).reshape(g, 128, n, -1)
    if fmt == "e4m3":
        vals = words.view(ml_dtypes.float8_e4m3fn).astype(np.float64)
    else:
        nib = np.empty((g, 128, n, 4), np.uint8)
        nib[..., 0::2] = words & 0xF
        nib[..., 1::2] = words >> 4
        vals = E2M1[nib]
    vals = vals * np.repeat(np.exp2(scales.astype(np.float64) - 127.0), 8, axis=1)[..., None]
    return vals.transpose(0, 1, 3, 2).reshape(g * 512, n)


def gelu(v):
    return 0.5 * v * (1.0 + np.tanh(np.sqrt(2.0 / np.pi) * (v + 0.044715 * v**3)))


K, T, S, H, N = 1536, 4096, 1024, 512, 384

def setup_inputs():
    n = np.random.standard_normal
    s = mx_kscale(K)[:, None]
    u = mx_kscale(H)[:, None]
    tab_words, tab_scales = pack_weight(n((K, T)) * s, "e4m3")
    ws_words, ws_scales = pack_weight(n((K, H)) / np.sqrt(K) / s, "e2m1")
    wf = n((K, H)) / np.sqrt(K) / s * u.T
    wj = 1.5 * n((H, N)) / np.sqrt(H) / u
    return {
        "tab_words": tab_words, "tab_scales": tab_scales,
        "offs": striped(np.random.permutation(T)[:S]),
        "wf": wf.astype(np.float32),
        "ws_words": ws_words, "ws_scales": ws_scales,
        "wj": wj.astype(np.float32),
        "bj": (0.5 * n(N)).astype(np.float32),
    }

def reference(tab_words, tab_scales, offs, wf, ws_words, ws_scales, wj, bj):
    v = unpack_weight(tab_words, tab_scales, "e4m3")[:, unstriped(offs)]
    wfq = mxq(f64(wf), 0, "e4m3")
    ws = unpack_weight(ws_words, ws_scales, "e2m1")
    force = wfq.T @ v
    stiff = ws.T @ v
    h = force / (1.0 + np.abs(stiff))
    hq = mxq(h, 0, "e4m3")
    wjq = mxq(f64(wj), 0, "e4m3")
    return (wjq.T @ hq) + f64(bj)[:, None]

@@ -1,0 +1,191 @@
+from contextlib import ExitStack
+
+import concourse.mybir as mybir
+
+K, T, S, H, N = 1536, 4096, 1024, 512, 384
+FLOPS = 2 * S * (2 * K * H + H * N)
+
+F32 = mybir.dt.float32
+BF16 = mybir.dt.bfloat16
+I32 = mybir.dt.int32
+U32 = mybir.dt.uint32
+U16 = mybir.dt.uint16
+U8 = mybir.dt.uint8
+FP8X4 = mybir.dt.float8_e4m3fn_x4
+FP4X4 = mybir.dt.float4_e2m1fn_x4
+ACT = mybir.ActivationFunctionType
+ALU = mybir.AluOpType
+
+P = 128
+PACK = 4
+PASSES = K // (P * PACK)
+BANKS = 8
+JB = S // BANKS
+CHUNKS = 4
+JC = S // CHUNKS
+N_TILES = N // P
+
+
+def tile_list_tactile_contact_torque_kernel(tc, tab_words, tab_scales, offs, wf, ws_words, ws_scales, wj, bj, out):
+    nc = tc.nc
+    with ExitStack() as ctx:
+        keep = ctx.enter_context(tc.tile_pool(name="keep", bufs=1))
+        psum = ctx.enter_context(tc.psum_pool(name="psum", bufs=1))
+
+        def sb(name, shape, dtype):
+            return keep.tile(shape, dtype, name=name, align_bytes=64)
+
+        offsets = keep.tile([P, S // 16], U16, name="offsets")
+        tab_w = [sb("tab_w%d" % a, [P, T], I32) for a in range(PASSES)]
+        tab_s = sb("tab_s", [P, PASSES, T // 4], I32)
+        v_w = [sb("v_w%d" % a, [P, S], U32) for a in range(PASSES)]
+        v_s = [sb("v_s%d" % a, [P, S], U8) for a in range(PASSES)]
+        ws_w_raw = sb("ws_w_raw", [P, PASSES, H // 2], I32)
+        ws_s_raw = sb("ws_s_raw", [P, PASSES, H // 4], I32)
+        ws_w = sb("ws_w", [P, PASSES, H // 2], I32)
+        ws_s = sb("ws_s", [P, PASSES, H // 4], I32)
+        wf_raw = [sb("wf_raw%d" % a, [P, PACK, H], F32) for a in range(PASSES)]
+        wf_bf = [sb("wf_bf%d" % a, [P, H * PACK], BF16) for a in range(PASSES)]
+        wf_w = [sb("wf_w%d" % a, [P, H], U32) for a in range(PASSES)]
+        wf_s = [sb("wf_s%d" % a, [P, H], U8) for a in range(PASSES)]
+        wj_raw = sb("wj_raw", [P, PACK, N], F32)
+        wj_bf = sb("wj_bf", [P, N * PACK], BF16)
+        wj_w = sb("wj_w", [P, N], U32)
+        wj_s = sb("wj_s", [P, N], U8)
+        bias = sb("bias", [P, N_TILES], F32)
+        warm = sb("warm", [P, 2], F32)
+        mag = [sb("mag%d" % c, [P, JC * PACK], F32) for c in range(CHUNKS)]
+        root = [sb("root%d" % c, [P, JC * PACK], F32) for c in range(CHUNKS)]
+        damp = [sb("damp%d" % c, [P, JC * PACK], F32) for c in range(CHUNKS)]
+        h_bf = [sb("h_bf%d" % c, [P, JC * PACK], BF16) for c in range(CHUNKS)]
+        h_w = [sb("h_w%d" % c, [P, JC], U32) for c in range(CHUNKS)]
+        h_s = [sb("h_s%d" % c, [P, JC], U8) for c in range(CHUNKS)]
+        res = [sb("res%d" % c, [P, N_TILES, JC], F32) for c in range(CHUNKS)]
+        banks = [psum.tile([P, PACK * JB], F32, name="bank%d" % b) for b in range(BANKS)]
+
+        nc.vector.memset(tab_s[:], 0)
+        nc.vector.memset(ws_s_raw[:], 0)
+        nc.gpsimd.memset(warm[:, 0:1], 1.0)
+        nc.scalar.activation(warm[:, 1:2], warm[:, 0:1], ACT.Abs_reciprocal_sqrt)
+
+        def load_table(a):
+            nc.sync.dma_start(tab_w[a][:], tab_words[a].rearrange("p t i -> p (t i)").bitcast(I32))
+
+        nc.sync.dma_start(offsets[:], offs)
+        nc.sync.dma_start(ws_w_raw[:], ws_words.bitcast(I32).rearrange("a p n -> p a n"))
+        load_table(0)
+        tab_scales_i = tab_scales.bitcast(I32).rearrange("a q n -> q a n")
+        for r in range(4):
+            nc.sync.dma_start(tab_s[r:P:32, :, :], tab_scales_i[r:16:4, :, :])
+        ws_scales_i = ws_scales.bitcast(I32).rearrange("a q n -> q a n")
+        for r in range(4):
+            nc.sync.dma_start(ws_s_raw[r:P:32, :, :], ws_scales_i[r:16:4, :, :])
+        load_table(1)
+        load_table(2)
+        for a in range(PASSES):
+            nc.sync.dma_start(wf_raw[a][:], wf[a * 512:(a + 1) * 512, :].rearrange("(p i) r -> p i r", i=PACK))
+        with nc.allow_non_contiguous_dma(reason="one bias value a partition"):
+            nc.sync.dma_start(bias[:], bj.rearrange("(c p) -> p c", p=P))
+        wj_rows = wj.rearrange("(q t e) n -> t q e n", t=PACK, e=8)
+        for t in range(PACK):
+            nc.sync.dma_start(wj_raw[:, t, :], wj_rows[t])
+
+        def gather_words(a, j0, j1):
+            nc.vector.tensor_copy(v_w[a][:, j0:j1], tab_w[a][:].bitcast(U32).indirect(offsets[:, j0 // 16:j1 // 16]))
+
+        def gather_scales(a):
+            nc.vector.tensor_copy(v_s[a][:], tab_s[:, a, :].bitcast(U8).indirect(offsets[:]))
+
+        def first_products(a, b, lhs, lhs_scale):
+            cols = slice(b * JB, (b + 1) * JB)
+            for t in range(PACK):
+                nc.tensor.matmul_mx(
+                    out=banks[b][:, t * JB:(t + 1) * JB], lhsT=lhs(t), lhsT_scale=lhs_scale(t),
+                    rhs=v_w[a][:, cols].bitcast(FP8X4), rhs_scale=v_s[a][:, cols],
+                    start=(a == 0 and t == 0), stop=(a == PASSES - 1 and t == PACK - 1))
+
+        def stiff(a, b):
+            first_products(a, b, lambda t: ws_w[:, a, t * 64:(t + 1) * 64].bitcast(FP4X4),
+                           lambda t: ws_s[:, a, t * 32:(t + 1) * 32].bitcast(U8))
+
+        def force(a, b):
+            first_products(a, b, lambda t: wf_w[a][:, t * P:(t + 1) * P].bitcast(FP8X4),
+                           lambda t: wf_s[a][:, t * P:(t + 1) * P])
+
+        def interleaved(b):
+            return banks[b][:].rearrange("p (t j) -> p j t", t=PACK)
+
+        def half(tile, b):
+            return tile[:, (b % 2) * 512:(b % 2 + 1) * 512].rearrange("p (j t) -> p j t", t=PACK)
+
+        gather_words(0, 0, S)
+        gather_scales(0)
+        nc.vector.tensor_copy(ws_w[:].rearrange("p a (t q w) -> p a t q w", t=PACK, w=4),
+                              ws_w_raw[:].rearrange("p a (q t w) -> p a t q w", t=PACK, w=4))
+        nc.vector.tensor_copy(ws_s[:].rearrange("p a (t q w) -> p a t q w", t=PACK, w=2),
+                              ws_s_raw[:].rearrange("p a (q t w) -> p a t q w", t=PACK, w=2))
+        for b in range(BANKS):
+            stiff(0, b)
+        gather_scales(1)
+        gather_words(1, 0, S)
+        for b in range(BANKS):
+            stiff(1, b)
+        gather_scales(2)
+        gather_words(2, 0, S // 2)
+        gather_words(2, S // 2, S)
+        for b in range(BANKS):
+            stiff(2, b)
+            nc.scalar.activation(half(mag[b // 2], b), interleaved(b), ACT.Abs)
+
+        def cast_wf(a, u):
+            nc.vector.tensor_copy(
+                wf_bf[a][:, u * 1024:(u + 1) * 1024].rearrange("p (t q e i) -> p t q e i", t=2, e=8, i=PACK),
+                wf_raw[a][:].rearrange("p i (q t e) -> p t q e i", t=PACK, e=8)[:, 2 * u:2 * u + 2])
+
+        def quant_wf(a, u):
+            nc.vector.quantize_mx(out=wf_w[a][:, u * 256:(u + 1) * 256].bitcast(FP8X4), scales=wf_s[a][:, u * 256:(u + 1) * 256],
+                                  in_=wf_bf[a][:, u * 1024:(u + 1) * 1024])
+
+        for a in range(PASSES):
+            cast_wf(a, 0)
+            cast_wf(a, 1)
+            quant_wf(a, 0)
+            quant_wf(a, 1)
+            for b in range(BANKS):
+                force(a, b)
+
+        for c in range(CHUNKS):
+            nc.scalar.activation(root[c][:], mag[c][:], ACT.Abs_reciprocal_sqrt, bias=1.0)
+            nc.scalar.activation(damp[c][:], root[c][:], ACT.Square)
+
+        nc.vector.tensor_copy(wj_bf[:].rearrange("p (n t) -> p n t", t=PACK), wj_raw[:].rearrange("p t n -> p n t"))
+
+        def multiply(c):
+            for b in (2 * c, 2 * c + 1):
+                nc.vector.tensor_tensor(half(h_bf[c], b), interleaved(b), half(damp[c], b), ALU.mult)
+
+        def quant_h(c):
+            nc.vector.quantize_mx(out=h_w[c][:].bitcast(FP8X4), scales=h_s[c][:], in_=h_bf[c][:])
+
+        def place(c, n):
+            return banks[2 * c + n // 2][:, (n % 2) * JC:(n % 2 + 1) * JC]
+
+        def finish(c):
+            for n in range(N_TILES):
+                nc.tensor.matmul_mx(out=place(c, n), lhsT=wj_w[:, n * P:(n + 1) * P].bitcast(FP8X4), lhsT_scale=wj_s[:, n * P:(n + 1) * P],
+                                    rhs=h_w[c][:].bitcast(FP8X4), rhs_scale=h_s[c][:], start=True, stop=True)
+            for n in range(N_TILES):
+                if c == CHUNKS - 1 and n == 2:
+                    nc.vector.tensor_scalar(res[c][:, n, :], place(c, n), bias[:, n:n + 1], None, ALU.add)
+                else:
+                    nc.scalar.activation(res[c][:, n, :], place(c, n), ACT.Identity, bias=bias[:, n:n + 1])
+            nc.sync.dma_start(out.rearrange("(n p) j -> p n j", p=P)[:, :, c * JC:(c + 1) * JC], res[c][:])
+
+        multiply(0)
+        nc.vector.quantize_mx(out=wj_w[:, 0:256].bitcast(FP8X4), scales=wj_s[:, 0:256], in_=wj_bf[:, 0:1024])
+        nc.vector.quantize_mx(out=wj_w[:, 256:384].bitcast(FP8X4), scales=wj_s[:, 256:384], in_=wj_bf[:, 1024:1536])
+        for c in range(CHUNKS):
+            quant_h(c)
+            if c + 1 < CHUNKS:
+                multiply(c + 1)
+            finish(c)

@@ -36,23 +36,31 @@ def tile_list_tactile_contact_torque_kernel(tc, tab_words, tab_scales, offs, wf,
             return keep.tile(shape, dtype, name=name, align_bytes=64)
 
         offsets = keep.tile([P, S // 16], U16, name="offsets")
-        tab_w = [sb("tab_w%d" % a, [P, T], I32) for a in range(PASSES)]
-        tab_s = sb("tab_s", [P, PASSES, T // 4], I32)
-        v_w = [sb("v_w%d" % a, [P, S], U32) for a in range(PASSES)]
         v_s = [sb("v_s%d" % a, [P, S], U8) for a in range(PASSES)]
-        ws_w_raw = sb("ws_w_raw", [P, PASSES, H // 2], I32)
-        ws_s_raw = sb("ws_s_raw", [P, PASSES, H // 4], I32)
+
+        def landing(name, shape, dtype, slot):
+            return keep.tile(shape, dtype, name=name, tag="landing%d" % slot, align_bytes=64)
+
+        ws_w_raw = landing("ws_w_raw", [P, PASSES, H // 2], I32, 1)
+        ws_s_raw = landing("ws_s_raw", [P, PASSES, H // 4], I32, 2)
+        tab_s_first = sb("tab_s_first", [P, T // 4], I32)
+        tab_s_later = sb("tab_s_later", [P, PASSES - 1, T // 4], I32)
+        tab_s = [tab_s_first[:]] + [tab_s_later[:, a, :] for a in range(PASSES - 1)]
+        tab_all = landing("tab_all", [P, PASSES, T], I32, 1)
+        tab_w = [tab_all[:, a, :] for a in range(PASSES)]
+        late = landing("late", [P, PACK * (PASSES * H + N) + N_TILES], F32, 2)
+        wf_raw = [late[:, a * PACK * H:(a + 1) * PACK * H].rearrange("p (i r) -> p i r", i=PACK) for a in range(PASSES)]
+        wj_raw = late[:, PACK * PASSES * H:PACK * (PASSES * H + N)].rearrange("p (t n) -> p t n", t=PACK)
+        bias = late[:, PACK * (PASSES * H + N):PACK * (PASSES * H + N) + N_TILES]
+        v_w = [sb("v_w%d" % a, [P, S], U32) for a in range(PASSES)]
         ws_w = sb("ws_w", [P, PASSES, H // 2], I32)
         ws_s = sb("ws_s", [P, PASSES, H // 4], I32)
-        wf_raw = [sb("wf_raw%d" % a, [P, PACK, H], F32) for a in range(PASSES)]
         wf_bf = [sb("wf_bf%d" % a, [P, H * PACK], BF16) for a in range(PASSES)]
         wf_w = [sb("wf_w%d" % a, [P, H], U32) for a in range(PASSES)]
         wf_s = [sb("wf_s%d" % a, [P, H], U8) for a in range(PASSES)]
-        wj_raw = sb("wj_raw", [P, PACK, N], F32)
         wj_bf = sb("wj_bf", [P, N * PACK], BF16)
         wj_w = sb("wj_w", [P, N], U32)
         wj_s = sb("wj_s", [P, N], U8)
-        bias = sb("bias", [P, N_TILES], F32)
         warm = sb("warm", [P, 2], F32)
         mag = [sb("mag%d" % c, [P, JC * PACK], F32) for c in range(CHUNKS)]
         root = [sb("root%d" % c, [P, JC * PACK], F32) for c in range(CHUNKS)]
@@ -63,38 +71,38 @@ def tile_list_tactile_contact_torque_kernel(tc, tab_words, tab_scales, offs, wf,
         res = [sb("res%d" % c, [P, N_TILES, JC], F32) for c in range(CHUNKS)]
         banks = [psum.tile([P, PACK * JB], F32, name="bank%d" % b) for b in range(BANKS)]
 
-        nc.vector.memset(tab_s[:], 0)
+        nc.vector.memset(tab_s_first[:], 0)
+        nc.vector.memset(tab_s_later[:], 0)
         nc.vector.memset(ws_s_raw[:], 0)
         nc.gpsimd.memset(warm[:, 0:1], 1.0)
         nc.scalar.activation(warm[:, 1:2], warm[:, 0:1], ACT.Abs_reciprocal_sqrt)
 
         def load_table(a):
-            nc.sync.dma_start(tab_w[a][:], tab_words[a].rearrange("p t i -> p (t i)").bitcast(I32))
+            nc.sync.dma_start(tab_w[a], tab_words[a].rearrange("p t i -> p (t i)").bitcast(I32))
 
         nc.sync.dma_start(offsets[:], offs)
         nc.sync.dma_start(ws_w_raw[:], ws_words.bitcast(I32).rearrange("a p n -> p a n"))
-        load_table(0)
+        ws_scales_i = ws_scales.bitcast(I32).rearrange("a q n -> q a n")
         tab_scales_i = tab_scales.bitcast(I32).rearrange("a q n -> q a n")
         for r in range(4):
-            nc.sync.dma_start(tab_s[r:P:32, :, :], tab_scales_i[r:16:4, :, :])
-        ws_scales_i = ws_scales.bitcast(I32).rearrange("a q n -> q a n")
+            nc.sync.dma_start(tab_s_first[r:P:32, :], tab_scales_i[r:16:4, 0, :])
+        for r in range(4):
+            nc.sync.dma_start(tab_s_later[r:P:32, :, :], tab_scales_i[r:16:4, 1:PASSES, :])
         for r in range(4):
             nc.sync.dma_start(ws_s_raw[r:P:32, :, :], ws_scales_i[r:16:4, :, :])
-        load_table(1)
-        load_table(2)
+
+        nc.vector.tensor_copy(ws_w[:].rearrange("p a (t q w) -> p a t q w", t=PACK, w=4),
+                              ws_w_raw[:].rearrange("p a (q t w) -> p a t q w", t=PACK, w=4))
+        nc.vector.tensor_copy(ws_s[:].rearrange("p a (t q w) -> p a t q w", t=PACK, w=2),
+                              ws_s_raw[:].rearrange("p a (q t w) -> p a t q w", t=PACK, w=2))
         for a in range(PASSES):
-            nc.sync.dma_start(wf_raw[a][:], wf[a * 512:(a + 1) * 512, :].rearrange("(p i) r -> p i r", i=PACK))
-        with nc.allow_non_contiguous_dma(reason="one bias value a partition"):
-            nc.sync.dma_start(bias[:], bj.rearrange("(c p) -> p c", p=P))
-        wj_rows = wj.rearrange("(q t e) n -> t q e n", t=PACK, e=8)
-        for t in range(PACK):
-            nc.sync.dma_start(wj_raw[:, t, :], wj_rows[t])
+            load_table(a)
 
         def gather_words(a, j0, j1):
-            nc.vector.tensor_copy(v_w[a][:, j0:j1], tab_w[a][:].bitcast(U32).indirect(offsets[:, j0 // 16:j1 // 16]))
+            nc.vector.tensor_copy(v_w[a][:, j0:j1], tab_w[a].bitcast(U32).indirect(offsets[:, j0 // 16:j1 // 16]))
 
         def gather_scales(a):
-            nc.vector.tensor_copy(v_s[a][:], tab_s[:, a, :].bitcast(U8).indirect(offsets[:]))
+            nc.vector.tensor_copy(v_s[a][:], tab_s[a].bitcast(U8).indirect(offsets[:]))
 
         def first_products(a, b, lhs, lhs_scale):
             cols = slice(b * JB, (b + 1) * JB)
@@ -118,29 +126,34 @@ def tile_list_tactile_contact_torque_kernel(tc, tab_words, tab_scales, offs, wf,
         def half(tile, b):
             return tile[:, (b % 2) * 512:(b % 2 + 1) * 512].rearrange("p (j t) -> p j t", t=PACK)
 
+        for a in range(PASSES):
+            gather_scales(a)
         gather_words(0, 0, S)
-        gather_scales(0)
-        nc.vector.tensor_copy(ws_w[:].rearrange("p a (t q w) -> p a t q w", t=PACK, w=4),
-                              ws_w_raw[:].rearrange("p a (q t w) -> p a t q w", t=PACK, w=4))
-        nc.vector.tensor_copy(ws_s[:].rearrange("p a (t q w) -> p a t q w", t=PACK, w=2),
-                              ws_s_raw[:].rearrange("p a (q t w) -> p a t q w", t=PACK, w=2))
         for b in range(BANKS):
             stiff(0, b)
-        gather_scales(1)
-        gather_words(1, 0, S)
+        gather_words(1, 0, S // 2)
+        gather_words(1, S // 2, S)
         for b in range(BANKS):
             stiff(1, b)
-        gather_scales(2)
         gather_words(2, 0, S // 2)
         gather_words(2, S // 2, S)
         for b in range(BANKS):
             stiff(2, b)
             nc.scalar.activation(half(mag[b // 2], b), interleaved(b), ACT.Abs)
 
+        for a in range(PASSES):
+            nc.sync.dma_start(wf_raw[a], wf[a * 512:(a + 1) * 512, :].rearrange("(p i) r -> p i r", i=PACK))
+        wj_rows = wj.rearrange("(q t e) n -> t q e n", t=PACK, e=8)
+        for t in range(PACK):
+            nc.sync.dma_start(wj_raw[:, t, :], wj_rows[t])
+        with nc.allow_non_contiguous_dma(reason="one bias value a partition"):
+            nc.sync.dma_start(bias, bj.rearrange("(c p) -> p c", p=P))
+
         def cast_wf(a, u):
-            nc.vector.tensor_copy(
-                wf_bf[a][:, u * 1024:(u + 1) * 1024].rearrange("p (t q e i) -> p t q e i", t=2, e=8, i=PACK),
-                wf_raw[a][:].rearrange("p i (q t e) -> p t q e i", t=PACK, e=8)[:, 2 * u:2 * u + 2])
+            for t in (2 * u, 2 * u + 1):
+                nc.vector.tensor_copy(
+                    wf_bf[a][:, t * 512:(t + 1) * 512].rearrange("p (q c e i) -> p q c i e", c=2, e=4, i=PACK),
+                    wf_raw[a].rearrange("p i (q t c e) -> p t q c i e", t=PACK, c=2, e=4)[:, t])
 
         def quant_wf(a, u):
             nc.vector.quantize_mx(out=wf_w[a][:, u * 256:(u + 1) * 256].bitcast(FP8X4), scales=wf_s[a][:, u * 256:(u + 1) * 256],
@@ -158,11 +171,10 @@ def tile_list_tactile_contact_torque_kernel(tc, tab_words, tab_scales, offs, wf,
             nc.scalar.activation(root[c][:], mag[c][:], ACT.Abs_reciprocal_sqrt, bias=1.0)
             nc.scalar.activation(damp[c][:], root[c][:], ACT.Square)
 
-        nc.vector.tensor_copy(wj_bf[:].rearrange("p (n t) -> p n t", t=PACK), wj_raw[:].rearrange("p t n -> p n t"))
+        nc.vector.tensor_copy(wj_bf[:].rearrange("p (c e t) -> p c t e", e=4, t=PACK), wj_raw.rearrange("p t (c e) -> p c t e", e=4))
 
-        def multiply(c):
-            for b in (2 * c, 2 * c + 1):
-                nc.vector.tensor_tensor(half(h_bf[c], b), interleaved(b), half(damp[c], b), ALU.mult)
+        def multiply(b):
+            nc.vector.tensor_tensor(half(h_bf[b // 2], b), interleaved(b), half(damp[b // 2], b), ALU.mult)
 
         def quant_h(c):
             nc.vector.quantize_mx(out=h_w[c][:].bitcast(FP8X4), scales=h_s[c][:], in_=h_bf[c][:])
@@ -184,8 +196,11 @@ def tile_list_tactile_contact_torque_kernel(tc, tab_words, tab_scales, offs, wf,
         multiply(0)
         nc.vector.quantize_mx(out=wj_w[:, 0:256].bitcast(FP8X4), scales=wj_s[:, 0:256], in_=wj_bf[:, 0:1024])
         nc.vector.quantize_mx(out=wj_w[:, 256:384].bitcast(FP8X4), scales=wj_s[:, 256:384], in_=wj_bf[:, 1024:1536])
+        multiply(1)
         for c in range(CHUNKS):
+            if c + 1 < CHUNKS:
+                multiply(2 * c + 2)
             quant_h(c)
             if c + 1 < CHUNKS:
-                multiply(c + 1)
+                multiply(2 * c + 3)
             finish(c)

@@ -24,6 +24,8 @@ JB = S // BANKS
 CHUNKS = 4
 JC = S // CHUNKS
 N_TILES = N // P
+ROWS = 16 * PASSES
+ROW0 = 48
 
 
 def tile_list_tactile_contact_torque_kernel(tc, tab_words, tab_scales, offs, wf, ws_words, ws_scales, wj, bj, out):
@@ -36,18 +38,16 @@ def tile_list_tactile_contact_torque_kernel(tc, tab_words, tab_scales, offs, wf,
             return keep.tile(shape, dtype, name=name, align_bytes=64)
 
         offsets = keep.tile([P, S // 16], U16, name="offsets")
-        v_s = [sb("v_s%d" % a, [P, S], U8) for a in range(PASSES)]
+        v_s = sb("v_s", [P, PASSES * S], U8)
 
         def landing(name, shape, dtype, slot):
             return keep.tile(shape, dtype, name=name, tag="landing%d" % slot, align_bytes=64)
 
         ws_w_raw = landing("ws_w_raw", [P, PASSES, H // 2], I32, 1)
-        ws_s_raw = landing("ws_s_raw", [P, PASSES, H // 4], I32, 2)
-        tab_s_first = sb("tab_s_first", [P, T // 4], I32)
-        tab_s_later = sb("tab_s_later", [P, PASSES - 1, T // 4], I32)
-        tab_s = [tab_s_first[:]] + [tab_s_later[:, a, :] for a in range(PASSES - 1)]
-        tab_all = landing("tab_all", [P, PASSES, T], I32, 1)
-        tab_w = [tab_all[:, a, :] for a in range(PASSES)]
+        ws_s_raw = sb("ws_s_raw", [P, PASSES, H // 4], I32)
+        tab_s = sb("tab_s", [P, T // 4], I32)
+        tab_w = [landing("tab_w%d" % a, [P, T], I32, a % 2)[:] for a in range(PASSES)]
+        picked_s = landing("picked_s", [P, S], U8, 2)
         late = landing("late", [P, PACK * (PASSES * H + N) + N_TILES], F32, 2)
         wf_raw = [late[:, a * PACK * H:(a + 1) * PACK * H].rearrange("p (i r) -> p i r", i=PACK) for a in range(PASSES)]
         wj_raw = late[:, PACK * PASSES * H:PACK * (PASSES * H + N)].rearrange("p (t n) -> p t n", t=PACK)
@@ -71,45 +71,45 @@ def tile_list_tactile_contact_torque_kernel(tc, tab_words, tab_scales, offs, wf,
         res = [sb("res%d" % c, [P, N_TILES, JC], F32) for c in range(CHUNKS)]
         banks = [psum.tile([P, PACK * JB], F32, name="bank%d" % b) for b in range(BANKS)]
 
-        nc.vector.memset(tab_s_first[:], 0)
-        nc.vector.memset(tab_s_later[:], 0)
         nc.vector.memset(ws_s_raw[:], 0)
-        nc.gpsimd.memset(warm[:, 0:1], 1.0)
-        nc.scalar.activation(warm[:, 1:2], warm[:, 0:1], ACT.Abs_reciprocal_sqrt)
+        nc.vector.memset(tab_s[0:ROW0, :], 0)
+        nc.vector.memset(tab_s[ROW0 + ROWS:P, :], 0)
+        nc.vector.memset(v_s[:].bitcast(I32), 0)
 
         def load_table(a):
             nc.sync.dma_start(tab_w[a], tab_words[a].rearrange("p t i -> p (t i)").bitcast(I32))
 
         nc.sync.dma_start(offsets[:], offs)
-        nc.sync.dma_start(ws_w_raw[:], ws_words.bitcast(I32).rearrange("a p n -> p a n"))
         ws_scales_i = ws_scales.bitcast(I32).rearrange("a q n -> q a n")
         tab_scales_i = tab_scales.bitcast(I32).rearrange("a q n -> q a n")
+        for a in range(PASSES):
+            nc.sync.dma_start(tab_s[ROW0 + a:ROW0 + ROWS:PASSES, :], tab_scales_i[:, a, :])
+        nc.sync.dma_start(ws_w_raw[:], ws_words.bitcast(I32).rearrange("a p n -> p a n"))
+        load_table(0)
         for r in range(4):
-            nc.sync.dma_start(tab_s_first[r:P:32, :], tab_scales_i[r:16:4, 0, :])
-        for r in range(4):
-            nc.sync.dma_start(tab_s_later[r:P:32, :, :], tab_scales_i[r:16:4, 1:PASSES, :])
-        for r in range(4):
-            nc.sync.dma_start(ws_s_raw[r:P:32, :, :], ws_scales_i[r:16:4, :, :])
+            nc.scalar.dma_start(ws_s_raw[r:P:32, :, :], ws_scales_i[r:16:4, :, :])
+        nc.gpsimd.memset(warm[:, 0:1], 1.0)
+        nc.scalar.activation(warm[:, 1:2], warm[:, 0:1], ACT.Abs_reciprocal_sqrt)
 
         nc.vector.tensor_copy(ws_w[:].rearrange("p a (t q w) -> p a t q w", t=PACK, w=4),
                               ws_w_raw[:].rearrange("p a (q t w) -> p a t q w", t=PACK, w=4))
+        load_table(1)
+        nc.vector.tensor_copy(picked_s[:], tab_s[:].bitcast(U8).indirect(offsets[:]))
+        for quad in range(4):
+            row = ROW0 + quad * 4 * PASSES
+            nc.scalar.dma_start(v_s[32 * quad:32 * quad + 4, :].bitcast(I32), picked_s[row:row + 4 * PASSES, :].bitcast(I32))
         nc.vector.tensor_copy(ws_s[:].rearrange("p a (t q w) -> p a t q w", t=PACK, w=2),
                               ws_s_raw[:].rearrange("p a (q t w) -> p a t q w", t=PACK, w=2))
-        for a in range(PASSES):
-            load_table(a)
 
         def gather_words(a, j0, j1):
             nc.vector.tensor_copy(v_w[a][:, j0:j1], tab_w[a].bitcast(U32).indirect(offsets[:, j0 // 16:j1 // 16]))
-
-        def gather_scales(a):
-            nc.vector.tensor_copy(v_s[a][:], tab_s[a].bitcast(U8).indirect(offsets[:]))
 
         def first_products(a, b, lhs, lhs_scale):
             cols = slice(b * JB, (b + 1) * JB)
             for t in range(PACK):
                 nc.tensor.matmul_mx(
                     out=banks[b][:, t * JB:(t + 1) * JB], lhsT=lhs(t), lhsT_scale=lhs_scale(t),
-                    rhs=v_w[a][:, cols].bitcast(FP8X4), rhs_scale=v_s[a][:, cols],
+                    rhs=v_w[a][:, cols].bitcast(FP8X4), rhs_scale=v_s[:, a * S + b * JB:a * S + (b + 1) * JB],
                     start=(a == 0 and t == 0), stop=(a == PASSES - 1 and t == PACK - 1))
 
         def stiff(a, b):
@@ -126,9 +126,8 @@ def tile_list_tactile_contact_torque_kernel(tc, tab_words, tab_scales, offs, wf,
         def half(tile, b):
             return tile[:, (b % 2) * 512:(b % 2 + 1) * 512].rearrange("p (j t) -> p j t", t=PACK)
 
-        for a in range(PASSES):
-            gather_scales(a)
         gather_words(0, 0, S)
+        load_table(2)
         for b in range(BANKS):
             stiff(0, b)
         gather_words(1, 0, S // 2)
@@ -164,7 +163,8 @@ def tile_list_tactile_contact_torque_kernel(tc, tab_words, tab_scales, offs, wf,
             cast_wf(a, 1)
             quant_wf(a, 0)
             quant_wf(a, 1)
-            for b in range(BANKS):
+        for b in range(BANKS):
+            for a in range(PASSES):
                 force(a, b)
 
         for c in range(CHUNKS):

@@ -38,23 +38,23 @@ def tile_list_tactile_contact_torque_kernel(tc, tab_words, tab_scales, offs, wf,
             return keep.tile(shape, dtype, name=name, align_bytes=64)
 
         offsets = keep.tile([P, S // 16], U16, name="offsets")
-        v_s = sb("v_s", [P, PASSES * S], U8)
+        planes = sb("planes", [P, PASSES * (S + H)], U8)
+        picked_s = sb("picked_s", [P, S], U8)
 
         def landing(name, shape, dtype, slot):
             return keep.tile(shape, dtype, name=name, tag="landing%d" % slot, align_bytes=64)
 
-        ws_w_raw = landing("ws_w_raw", [P, PASSES, H // 2], I32, 1)
-        ws_s_raw = sb("ws_s_raw", [P, PASSES, H // 4], I32)
+        ws_w_raw = sb("ws_w_raw", [P, PASSES, H // 2], I32)
+        ws_s_raw = sb("ws_s_raw", [P, H // 4], I32)
         tab_s = sb("tab_s", [P, T // 4], I32)
-        tab_w = [landing("tab_w%d" % a, [P, T], I32, a % 2)[:] for a in range(PASSES)]
-        picked_s = landing("picked_s", [P, S], U8, 2)
+        tab_w = [sb("tab_w%d" % a, [P, T], I32)[:] for a in range(PASSES)]
+        staged = landing("staged", [P, (S + H) // 4], I32, 2)
         late = landing("late", [P, PACK * (PASSES * H + N) + N_TILES], F32, 2)
         wf_raw = [late[:, a * PACK * H:(a + 1) * PACK * H].rearrange("p (i r) -> p i r", i=PACK) for a in range(PASSES)]
         wj_raw = late[:, PACK * PASSES * H:PACK * (PASSES * H + N)].rearrange("p (t n) -> p t n", t=PACK)
         bias = late[:, PACK * (PASSES * H + N):PACK * (PASSES * H + N) + N_TILES]
         v_w = [sb("v_w%d" % a, [P, S], U32) for a in range(PASSES)]
         ws_w = sb("ws_w", [P, PASSES, H // 2], I32)
-        ws_s = sb("ws_s", [P, PASSES, H // 4], I32)
         wf_bf = [sb("wf_bf%d" % a, [P, H * PACK], BF16) for a in range(PASSES)]
         wf_w = [sb("wf_w%d" % a, [P, H], U32) for a in range(PASSES)]
         wf_s = [sb("wf_s%d" % a, [P, H], U8) for a in range(PASSES)]
@@ -71,10 +71,10 @@ def tile_list_tactile_contact_torque_kernel(tc, tab_words, tab_scales, offs, wf,
         res = [sb("res%d" % c, [P, N_TILES, JC], F32) for c in range(CHUNKS)]
         banks = [psum.tile([P, PACK * JB], F32, name="bank%d" % b) for b in range(BANKS)]
 
-        nc.vector.memset(ws_s_raw[:], 0)
-        nc.vector.memset(tab_s[0:ROW0, :], 0)
-        nc.vector.memset(tab_s[ROW0 + ROWS:P, :], 0)
-        nc.vector.memset(v_s[:].bitcast(I32), 0)
+        for rows in (slice(0, ROW0), slice(ROW0 + ROWS, P)):
+            nc.vector.memset(tab_s[rows, :], 0)
+            nc.vector.memset(ws_s_raw[rows, :], 0)
+        nc.vector.memset(planes[:].bitcast(I32), 0)
 
         def load_table(a):
             nc.sync.dma_start(tab_w[a], tab_words[a].rearrange("p t i -> p (t i)").bitcast(I32))
@@ -85,21 +85,21 @@ def tile_list_tactile_contact_torque_kernel(tc, tab_words, tab_scales, offs, wf,
         for a in range(PASSES):
             nc.sync.dma_start(tab_s[ROW0 + a:ROW0 + ROWS:PASSES, :], tab_scales_i[:, a, :])
         nc.sync.dma_start(ws_w_raw[:], ws_words.bitcast(I32).rearrange("a p n -> p a n"))
-        load_table(0)
-        for r in range(4):
-            nc.scalar.dma_start(ws_s_raw[r:P:32, :, :], ws_scales_i[r:16:4, :, :])
+        nc.scalar.dma_start(ws_s_raw[ROW0:ROW0 + ROWS, :], ws_scales_i)
+        for a in range(PASSES):
+            load_table(a)
         nc.gpsimd.memset(warm[:, 0:1], 1.0)
         nc.scalar.activation(warm[:, 1:2], warm[:, 0:1], ACT.Abs_reciprocal_sqrt)
 
-        nc.vector.tensor_copy(ws_w[:].rearrange("p a (t q w) -> p a t q w", t=PACK, w=4),
-                              ws_w_raw[:].rearrange("p a (q t w) -> p a t q w", t=PACK, w=4))
-        load_table(1)
         nc.vector.tensor_copy(picked_s[:], tab_s[:].bitcast(U8).indirect(offsets[:]))
+        nc.vector.tensor_copy(staged[:, S // 4:].rearrange("p (t q w) -> p t q w", t=PACK, w=2),
+                              ws_s_raw[:].rearrange("p (q t w) -> p t q w", t=PACK, w=2))
+        nc.vector.tensor_copy(staged[:, 0:S // 4], picked_s[:].bitcast(I32))
         for quad in range(4):
             row = ROW0 + quad * 4 * PASSES
-            nc.scalar.dma_start(v_s[32 * quad:32 * quad + 4, :].bitcast(I32), picked_s[row:row + 4 * PASSES, :].bitcast(I32))
-        nc.vector.tensor_copy(ws_s[:].rearrange("p a (t q w) -> p a t q w", t=PACK, w=2),
-                              ws_s_raw[:].rearrange("p a (q t w) -> p a t q w", t=PACK, w=2))
+            nc.scalar.dma_start(planes[32 * quad:32 * quad + 4, :].bitcast(I32), staged[row:row + 4 * PASSES, :])
+        nc.vector.tensor_copy(ws_w[:].rearrange("p a (t q w) -> p a t q w", t=PACK, w=4),
+                              ws_w_raw[:].rearrange("p a (q t w) -> p a t q w", t=PACK, w=4))
 
         def gather_words(a, j0, j1):
             nc.vector.tensor_copy(v_w[a][:, j0:j1], tab_w[a].bitcast(U32).indirect(offsets[:, j0 // 16:j1 // 16]))
@@ -109,12 +109,12 @@ def tile_list_tactile_contact_torque_kernel(tc, tab_words, tab_scales, offs, wf,
             for t in range(PACK):
                 nc.tensor.matmul_mx(
                     out=banks[b][:, t * JB:(t + 1) * JB], lhsT=lhs(t), lhsT_scale=lhs_scale(t),
-                    rhs=v_w[a][:, cols].bitcast(FP8X4), rhs_scale=v_s[:, a * S + b * JB:a * S + (b + 1) * JB],
+                    rhs=v_w[a][:, cols].bitcast(FP8X4), rhs_scale=planes[:, a * (S + H) + b * JB:a * (S + H) + (b + 1) * JB],
                     start=(a == 0 and t == 0), stop=(a == PASSES - 1 and t == PACK - 1))
 
         def stiff(a, b):
             first_products(a, b, lambda t: ws_w[:, a, t * 64:(t + 1) * 64].bitcast(FP4X4),
-                           lambda t: ws_s[:, a, t * 32:(t + 1) * 32].bitcast(U8))
+                           lambda t: planes[:, a * (S + H) + S + t * P:a * (S + H) + S + (t + 1) * P])
 
         def force(a, b):
             first_products(a, b, lambda t: wf_w[a][:, t * P:(t + 1) * P].bitcast(FP8X4),
@@ -127,7 +127,6 @@ def tile_list_tactile_contact_torque_kernel(tc, tab_words, tab_scales, offs, wf,
             return tile[:, (b % 2) * 512:(b % 2 + 1) * 512].rearrange("p (j t) -> p j t", t=PACK)
 
         gather_words(0, 0, S)
-        load_table(2)
         for b in range(BANKS):
             stiff(0, b)
         gather_words(1, 0, S // 2)
@@ -163,8 +162,8 @@ def tile_list_tactile_contact_torque_kernel(tc, tab_words, tab_scales, offs, wf,
             cast_wf(a, 1)
             quant_wf(a, 0)
             quant_wf(a, 1)
-        for b in range(BANKS):
-            for a in range(PASSES):
+        for a in range(PASSES):
+            for b in range(BANKS):
                 force(a, b)
 
         for c in range(CHUNKS):

@@ -21,8 +21,7 @@ PACK = 4
 PASSES = K // (P * PACK)
 BANKS = 8
 JB = S // BANKS
-CHUNKS = 4
-JC = S // CHUNKS
+CHUNKS = ((0, 2), (2, 2), (4, 2), (6, 1), (7, 1))
 N_TILES = N // P
 ROWS = 16 * PASSES
 ROW0 = 48
@@ -38,8 +37,9 @@ def tile_list_tactile_contact_torque_kernel(tc, tab_words, tab_scales, offs, wf,
             return keep.tile(shape, dtype, name=name, align_bytes=64)
 
         offsets = keep.tile([P, S // 16], U16, name="offsets")
-        planes = sb("planes", [P, PASSES * (S + H)], U8)
-        picked_s = sb("picked_s", [P, S], U8)
+        planes_early = sb("planes_early", [P, 2, S + H], U8)
+        planes_last = sb("planes_last", [P, S + H], U8)
+        planes = [planes_early[:, 0, :], planes_early[:, 1, :], planes_last[:]]
 
         def landing(name, shape, dtype, slot):
             return keep.tile(shape, dtype, name=name, tag="landing%d" % slot, align_bytes=64)
@@ -47,7 +47,10 @@ def tile_list_tactile_contact_torque_kernel(tc, tab_words, tab_scales, offs, wf,
         ws_w_raw = sb("ws_w_raw", [P, PASSES, H // 2], I32)
         ws_s_raw = sb("ws_s_raw", [P, H // 4], I32)
         tab_s = sb("tab_s", [P, T // 4], I32)
-        tab_w = [sb("tab_w%d" % a, [P, T], I32)[:] for a in range(PASSES)]
+        tab_first = sb("tab_first", [P, T], I32)
+        picked_s = landing("picked_s", [P, S], U8, 1)
+        tab_later = landing("tab_later", [P, PASSES - 1, T], I32, 1)
+        tab_w = [tab_first[:]] + [tab_later[:, a, :] for a in range(PASSES - 1)]
         staged = landing("staged", [P, (S + H) // 4], I32, 2)
         late = landing("late", [P, PACK * (PASSES * H + N) + N_TILES], F32, 2)
         wf_raw = [late[:, a * PACK * H:(a + 1) * PACK * H].rearrange("p (i r) -> p i r", i=PACK) for a in range(PASSES)]
@@ -62,19 +65,22 @@ def tile_list_tactile_contact_torque_kernel(tc, tab_words, tab_scales, offs, wf,
         wj_w = sb("wj_w", [P, N], U32)
         wj_s = sb("wj_s", [P, N], U8)
         warm = sb("warm", [P, 2], F32)
-        mag = [sb("mag%d" % c, [P, JC * PACK], F32) for c in range(CHUNKS)]
-        root = [sb("root%d" % c, [P, JC * PACK], F32) for c in range(CHUNKS)]
-        damp = [sb("damp%d" % c, [P, JC * PACK], F32) for c in range(CHUNKS)]
-        h_bf = [sb("h_bf%d" % c, [P, JC * PACK], BF16) for c in range(CHUNKS)]
-        h_w = [sb("h_w%d" % c, [P, JC], U32) for c in range(CHUNKS)]
-        h_s = [sb("h_s%d" % c, [P, JC], U8) for c in range(CHUNKS)]
-        res = [sb("res%d" % c, [P, N_TILES, JC], F32) for c in range(CHUNKS)]
+        widths = [count * JB for first, count in CHUNKS]
+        mag = [sb("mag%d" % c, [P, w * PACK], F32) for c, w in enumerate(widths)]
+        root = [sb("root%d" % c, [P, w * PACK], F32) for c, w in enumerate(widths)]
+        damp = [sb("damp%d" % c, [P, w * PACK], F32) for c, w in enumerate(widths)]
+        h_bf = [sb("h_bf%d" % c, [P, w * PACK], BF16) for c, w in enumerate(widths)]
+        h_w = [sb("h_w%d" % c, [P, w], U32) for c, w in enumerate(widths)]
+        h_s = [sb("h_s%d" % c, [P, w], U8) for c, w in enumerate(widths)]
+        res = [sb("res%d" % c, [P, N_TILES, w], F32) for c, w in enumerate(widths)]
         banks = [psum.tile([P, PACK * JB], F32, name="bank%d" % b) for b in range(BANKS)]
 
+        nc.vector.memset(tab_s[0:ROW0, :], 0)
+        nc.gpsimd.memset(tab_s[ROW0 + ROWS:P, :], 0)
         for rows in (slice(0, ROW0), slice(ROW0 + ROWS, P)):
-            nc.vector.memset(tab_s[rows, :], 0)
-            nc.vector.memset(ws_s_raw[rows, :], 0)
-        nc.vector.memset(planes[:].bitcast(I32), 0)
+            nc.gpsimd.memset(ws_s_raw[rows, :], 0)
+        nc.vector.memset(planes_early[:].bitcast(I32), 0)
+        nc.gpsimd.memset(planes_last[:].bitcast(I32), 0)
 
         def load_table(a):
             nc.sync.dma_start(tab_w[a], tab_words[a].rearrange("p t i -> p (t i)").bitcast(I32))
@@ -82,49 +88,56 @@ def tile_list_tactile_contact_torque_kernel(tc, tab_words, tab_scales, offs, wf,
         nc.sync.dma_start(offsets[:], offs)
         ws_scales_i = ws_scales.bitcast(I32).rearrange("a q n -> q a n")
         tab_scales_i = tab_scales.bitcast(I32).rearrange("a q n -> q a n")
-        for a in range(PASSES):
-            nc.sync.dma_start(tab_s[ROW0 + a:ROW0 + ROWS:PASSES, :], tab_scales_i[:, a, :])
+        for rows_sb, rows_hbm in ((tab_s, tab_scales_i), (ws_s_raw, ws_scales_i)):
+            nc.sync.dma_start(rows_sb[ROW0:ROW0 + 32, :], rows_hbm[:, 0:2, :])
+            nc.sync.dma_start(rows_sb[ROW0 + 32:ROW0 + ROWS, :], rows_hbm[:, 2, :])
         nc.sync.dma_start(ws_w_raw[:], ws_words.bitcast(I32).rearrange("a p n -> p a n"))
-        nc.scalar.dma_start(ws_s_raw[ROW0:ROW0 + ROWS, :], ws_scales_i)
-        for a in range(PASSES):
-            load_table(a)
+        load_table(0)
         nc.gpsimd.memset(warm[:, 0:1], 1.0)
         nc.scalar.activation(warm[:, 1:2], warm[:, 0:1], ACT.Abs_reciprocal_sqrt)
 
         nc.vector.tensor_copy(picked_s[:], tab_s[:].bitcast(U8).indirect(offsets[:]))
-        nc.vector.tensor_copy(staged[:, S // 4:].rearrange("p (t q w) -> p t q w", t=PACK, w=2),
-                              ws_s_raw[:].rearrange("p (q t w) -> p t q w", t=PACK, w=2))
+        nc.vector.tensor_copy(staged[:, S // 4:].rearrange("p (t g) -> p t g", t=PACK),
+                              ws_s_raw[:].rearrange("p (g t) -> p t g", t=PACK))
         nc.vector.tensor_copy(staged[:, 0:S // 4], picked_s[:].bitcast(I32))
         for quad in range(4):
-            row = ROW0 + quad * 4 * PASSES
-            nc.scalar.dma_start(planes[32 * quad:32 * quad + 4, :].bitcast(I32), staged[row:row + 4 * PASSES, :])
-        nc.vector.tensor_copy(ws_w[:].rearrange("p a (t q w) -> p a t q w", t=PACK, w=4),
-                              ws_w_raw[:].rearrange("p a (q t w) -> p a t q w", t=PACK, w=4))
+            row = ROW0 + quad * 8
+            queue = nc.scalar if quad % 2 else nc.sync
+            queue.dma_start(planes_early[32 * quad:32 * quad + 4, :, :].bitcast(I32), staged[row:row + 8, :])
+        load_table(1)
+        for quad in range(4):
+            row = ROW0 + 32 + quad * 4
+            nc.sync.dma_start(planes_last[32 * quad:32 * quad + 4, :].bitcast(I32), staged[row:row + 4, :])
+        load_table(2)
+        nc.vector.tensor_copy(ws_w[:].rearrange("p a (t g w) -> p a t g w", t=PACK, w=2),
+                              ws_w_raw[:].rearrange("p a (g t w) -> p a t g w", t=PACK, w=2))
 
         def gather_words(a, j0, j1):
             nc.vector.tensor_copy(v_w[a][:, j0:j1], tab_w[a].bitcast(U32).indirect(offsets[:, j0 // 16:j1 // 16]))
 
-        def first_products(a, b, lhs, lhs_scale):
+        def first_products(a, b, step, lhs, lhs_scale):
             cols = slice(b * JB, (b + 1) * JB)
             for t in range(PACK):
                 nc.tensor.matmul_mx(
                     out=banks[b][:, t * JB:(t + 1) * JB], lhsT=lhs(t), lhsT_scale=lhs_scale(t),
-                    rhs=v_w[a][:, cols].bitcast(FP8X4), rhs_scale=planes[:, a * (S + H) + b * JB:a * (S + H) + (b + 1) * JB],
-                    start=(a == 0 and t == 0), stop=(a == PASSES - 1 and t == PACK - 1))
+                    rhs=v_w[a][:, cols].bitcast(FP8X4), rhs_scale=planes[a][:, cols],
+                    start=(step == 0 and t == 0), stop=(step == PASSES - 1 and t == PACK - 1))
 
         def stiff(a, b):
-            first_products(a, b, lambda t: ws_w[:, a, t * 64:(t + 1) * 64].bitcast(FP4X4),
-                           lambda t: planes[:, a * (S + H) + S + t * P:a * (S + H) + S + (t + 1) * P])
+            first_products(a, b, a, lambda t: ws_w[:, a, t * 64:(t + 1) * 64].bitcast(FP4X4),
+                           lambda t: planes[a][:, S + t * P:S + (t + 1) * P])
 
-        def force(a, b):
-            first_products(a, b, lambda t: wf_w[a][:, t * P:(t + 1) * P].bitcast(FP8X4),
+        def force(a, b, step):
+            first_products(a, b, step, lambda t: wf_w[a][:, t * P:(t + 1) * P].bitcast(FP8X4),
                            lambda t: wf_s[a][:, t * P:(t + 1) * P])
 
         def interleaved(b):
             return banks[b][:].rearrange("p (t j) -> p j t", t=PACK)
 
-        def half(tile, b):
-            return tile[:, (b % 2) * 512:(b % 2 + 1) * 512].rearrange("p (j t) -> p j t", t=PACK)
+        def share(tiles, b):
+            c = max(i for i, (first, count) in enumerate(CHUNKS) if first <= b)
+            o = (b - CHUNKS[c][0]) * 512
+            return tiles[c][:, o:o + 512].rearrange("p (j t) -> p j t", t=PACK)
 
         gather_words(0, 0, S)
         for b in range(BANKS):
@@ -137,21 +150,20 @@ def tile_list_tactile_contact_torque_kernel(tc, tab_words, tab_scales, offs, wf,
         gather_words(2, S // 2, S)
         for b in range(BANKS):
             stiff(2, b)
-            nc.scalar.activation(half(mag[b // 2], b), interleaved(b), ACT.Abs)
+            nc.scalar.activation(share(mag, b), interleaved(b), ACT.Abs)
 
         for a in range(PASSES):
             nc.sync.dma_start(wf_raw[a], wf[a * 512:(a + 1) * 512, :].rearrange("(p i) r -> p i r", i=PACK))
-        wj_rows = wj.rearrange("(q t e) n -> t q e n", t=PACK, e=8)
+        wj_rows = wj.rearrange("(g t e) n -> t g e n", t=PACK, e=4)
         for t in range(PACK):
             nc.sync.dma_start(wj_raw[:, t, :], wj_rows[t])
         with nc.allow_non_contiguous_dma(reason="one bias value a partition"):
             nc.sync.dma_start(bias, bj.rearrange("(c p) -> p c", p=P))
 
         def cast_wf(a, u):
-            for t in (2 * u, 2 * u + 1):
-                nc.vector.tensor_copy(
-                    wf_bf[a][:, t * 512:(t + 1) * 512].rearrange("p (q c e i) -> p q c i e", c=2, e=4, i=PACK),
-                    wf_raw[a].rearrange("p i (q t c e) -> p t q c i e", t=PACK, c=2, e=4)[:, t])
+            nc.vector.tensor_copy(
+                wf_bf[a][:].rearrange("p (t g e i) -> p t g i e", t=PACK, e=4, i=PACK)[:, 2 * u:2 * u + 2],
+                wf_raw[a].rearrange("p i (g t e) -> p t g i e", t=PACK, e=4)[:, 2 * u:2 * u + 2])
 
         def quant_wf(a, u):
             nc.vector.quantize_mx(out=wf_w[a][:, u * 256:(u + 1) * 256].bitcast(FP8X4), scales=wf_s[a][:, u * 256:(u + 1) * 256],
@@ -162,44 +174,49 @@ def tile_list_tactile_contact_torque_kernel(tc, tab_words, tab_scales, offs, wf,
             cast_wf(a, 1)
             quant_wf(a, 0)
             quant_wf(a, 1)
-        for a in range(PASSES):
-            for b in range(BANKS):
-                force(a, b)
+        for b in range(BANKS):
+            for step, a in enumerate((0, 1, 2) if b < BANKS // 2 else (0, 2, 1)):
+                force(a, b, step)
 
-        for c in range(CHUNKS):
-            nc.scalar.activation(root[c][:], mag[c][:], ACT.Abs_reciprocal_sqrt, bias=1.0)
-            nc.scalar.activation(damp[c][:], root[c][:], ACT.Square)
+        for b in range(BANKS):
+            nc.scalar.activation(share(root, b), share(mag, b), ACT.Abs_reciprocal_sqrt, bias=1.0)
+            nc.scalar.activation(share(damp, b), share(root, b), ACT.Square)
 
         nc.vector.tensor_copy(wj_bf[:].rearrange("p (c e t) -> p c t e", e=4, t=PACK), wj_raw.rearrange("p t (c e) -> p c t e", e=4))
 
         def multiply(b):
-            nc.vector.tensor_tensor(half(h_bf[b // 2], b), interleaved(b), half(damp[b // 2], b), ALU.mult)
+            nc.vector.tensor_tensor(share(h_bf, b), interleaved(b), share(damp, b), ALU.mult)
 
         def quant_h(c):
             nc.vector.quantize_mx(out=h_w[c][:].bitcast(FP8X4), scales=h_s[c][:], in_=h_bf[c][:])
 
+        last = len(CHUNKS) - 1
+
         def place(c, n):
-            return banks[2 * c + n // 2][:, (n % 2) * JC:(n % 2 + 1) * JC]
+            first, count = CHUNKS[c]
+            w = widths[c]
+            if count == 2:
+                return banks[first + n // 2][:, (n % 2) * w:(n % 2 + 1) * w]
+            if c == last and n == 2:
+                return banks[1][:, 2 * JB:3 * JB]
+            return banks[first][:, n * w:(n + 1) * w]
 
         def finish(c):
+            j0 = CHUNKS[c][0] * JB
             for n in range(N_TILES):
                 nc.tensor.matmul_mx(out=place(c, n), lhsT=wj_w[:, n * P:(n + 1) * P].bitcast(FP8X4), lhsT_scale=wj_s[:, n * P:(n + 1) * P],
                                     rhs=h_w[c][:].bitcast(FP8X4), rhs_scale=h_s[c][:], start=True, stop=True)
             for n in range(N_TILES):
-                if c == CHUNKS - 1 and n == 2:
+                if c == 0 or (c == last and n == 2):
                     nc.vector.tensor_scalar(res[c][:, n, :], place(c, n), bias[:, n:n + 1], None, ALU.add)
                 else:
                     nc.scalar.activation(res[c][:, n, :], place(c, n), ACT.Identity, bias=bias[:, n:n + 1])
-            nc.sync.dma_start(out.rearrange("(n p) j -> p n j", p=P)[:, :, c * JC:(c + 1) * JC], res[c][:])
+            nc.sync.dma_start(out.rearrange("(n p) j -> p n j", p=P)[:, :, j0:j0 + widths[c]], res[c][:])
 
-        multiply(0)
         nc.vector.quantize_mx(out=wj_w[:, 0:256].bitcast(FP8X4), scales=wj_s[:, 0:256], in_=wj_bf[:, 0:1024])
         nc.vector.quantize_mx(out=wj_w[:, 256:384].bitcast(FP8X4), scales=wj_s[:, 256:384], in_=wj_bf[:, 1024:1536])
-        multiply(1)
-        for c in range(CHUNKS):
-            if c + 1 < CHUNKS:
-                multiply(2 * c + 2)
+        for c, (first, count) in enumerate(CHUNKS):
+            for b in range(first, first + count):
+                multiply(b)
             quant_h(c)
-            if c + 1 < CHUNKS:
-                multiply(2 * c + 3)
             finish(c)

@@ -131,13 +131,10 @@ def tile_list_tactile_contact_torque_kernel(tc, tab_words, tab_scales, offs, wf,
             first_products(a, b, step, lambda t: wf_w[a][:, t * P:(t + 1) * P].bitcast(FP8X4),
                            lambda t: wf_s[a][:, t * P:(t + 1) * P])
 
-        def interleaved(b):
-            return banks[b][:].rearrange("p (t j) -> p j t", t=PACK)
-
         def share(tiles, b):
             c = max(i for i, (first, count) in enumerate(CHUNKS) if first <= b)
             o = (b - CHUNKS[c][0]) * 512
-            return tiles[c][:, o:o + 512].rearrange("p (j t) -> p j t", t=PACK)
+            return tiles[c][:, o:o + 512]
 
         gather_words(0, 0, S)
         for b in range(BANKS):
@@ -150,7 +147,7 @@ def tile_list_tactile_contact_torque_kernel(tc, tab_words, tab_scales, offs, wf,
         gather_words(2, S // 2, S)
         for b in range(BANKS):
             stiff(2, b)
-            nc.scalar.activation(share(mag, b), interleaved(b), ACT.Abs)
+            nc.scalar.activation(share(mag, b), banks[b][:], ACT.Abs)
 
         for a in range(PASSES):
             nc.sync.dma_start(wf_raw[a], wf[a * 512:(a + 1) * 512, :].rearrange("(p i) r -> p i r", i=PACK))
@@ -185,7 +182,9 @@ def tile_list_tactile_contact_torque_kernel(tc, tab_words, tab_scales, offs, wf,
         nc.vector.tensor_copy(wj_bf[:].rearrange("p (c e t) -> p c t e", e=4, t=PACK), wj_raw.rearrange("p t (c e) -> p c t e", e=4))
 
         def multiply(b):
-            nc.vector.tensor_tensor(share(h_bf, b), interleaved(b), share(damp, b), ALU.mult)
+            nc.vector.tensor_tensor(share(h_bf, b).rearrange("p (c e t) -> p c t e", e=2, t=PACK),
+                                    banks[b][:].rearrange("p (t c e) -> p c t e", e=2, t=PACK),
+                                    share(damp, b).rearrange("p (t c e) -> p c t e", e=2, t=PACK), ALU.mult)
 
         def quant_h(c):
             nc.vector.quantize_mx(out=h_w[c][:].bitcast(FP8X4), scales=h_s[c][:], in_=h_bf[c][:])

@@ -66,7 +66,7 @@ def tile_list_tactile_contact_torque_kernel(tc, tab_words, tab_scales, offs, wf,
         wj_s = sb("wj_s", [P, N], U8)
         warm = sb("warm", [P, 2], F32)
         widths = [count * JB for first, count in CHUNKS]
-        mag = [sb("mag%d" % c, [P, w * PACK], F32) for c, w in enumerate(widths)]
+        mag = [sb("mag%d" % half, [P, PACK, 512], F32) for half in range(2)]
         root = [sb("root%d" % c, [P, w * PACK], F32) for c, w in enumerate(widths)]
         damp = [sb("damp%d" % c, [P, w * PACK], F32) for c, w in enumerate(widths)]
         h_bf = [sb("h_bf%d" % c, [P, w * PACK], BF16) for c, w in enumerate(widths)]
@@ -115,39 +115,35 @@ def tile_list_tactile_contact_torque_kernel(tc, tab_words, tab_scales, offs, wf,
         def gather_words(a, j0, j1):
             nc.vector.tensor_copy(v_w[a][:, j0:j1], tab_w[a].bitcast(U32).indirect(offsets[:, j0 // 16:j1 // 16]))
 
-        def first_products(a, b, step, lhs, lhs_scale):
+        def stiff(a, half):
+            cols = slice(half * 512, (half + 1) * 512)
+            for t in range(PACK):
+                nc.tensor.matmul_mx(
+                    out=banks[PACK * half + t][:], lhsT=ws_w[:, a, t * 64:(t + 1) * 64].bitcast(FP4X4),
+                    lhsT_scale=planes[a][:, S + t * P:S + (t + 1) * P],
+                    rhs=v_w[a][:, cols].bitcast(FP8X4), rhs_scale=planes[a][:, cols],
+                    start=(a == 0), stop=(a == PASSES - 1))
+
+        def force(a, b, step):
             cols = slice(b * JB, (b + 1) * JB)
             for t in range(PACK):
                 nc.tensor.matmul_mx(
-                    out=banks[b][:, t * JB:(t + 1) * JB], lhsT=lhs(t), lhsT_scale=lhs_scale(t),
+                    out=banks[b][:, t * JB:(t + 1) * JB], lhsT=wf_w[a][:, t * P:(t + 1) * P].bitcast(FP8X4),
+                    lhsT_scale=wf_s[a][:, t * P:(t + 1) * P],
                     rhs=v_w[a][:, cols].bitcast(FP8X4), rhs_scale=planes[a][:, cols],
                     start=(step == 0 and t == 0), stop=(step == PASSES - 1 and t == PACK - 1))
-
-        def stiff(a, b):
-            first_products(a, b, a, lambda t: ws_w[:, a, t * 64:(t + 1) * 64].bitcast(FP4X4),
-                           lambda t: planes[a][:, S + t * P:S + (t + 1) * P])
-
-        def force(a, b, step):
-            first_products(a, b, step, lambda t: wf_w[a][:, t * P:(t + 1) * P].bitcast(FP8X4),
-                           lambda t: wf_s[a][:, t * P:(t + 1) * P])
 
         def share(tiles, b):
             c = max(i for i, (first, count) in enumerate(CHUNKS) if first <= b)
             o = (b - CHUNKS[c][0]) * 512
             return tiles[c][:, o:o + 512]
 
-        gather_words(0, 0, S)
+        for a in range(PASSES):
+            for half in range(2):
+                gather_words(a, half * 512, (half + 1) * 512)
+                stiff(a, half)
         for b in range(BANKS):
-            stiff(0, b)
-        gather_words(1, 0, S // 2)
-        gather_words(1, S // 2, S)
-        for b in range(BANKS):
-            stiff(1, b)
-        gather_words(2, 0, S // 2)
-        gather_words(2, S // 2, S)
-        for b in range(BANKS):
-            stiff(2, b)
-            nc.scalar.activation(share(mag, b), banks[b][:], ACT.Abs)
+            nc.scalar.activation(mag[b // PACK][:, b % PACK, :], banks[b][:], ACT.Abs)
 
         for a in range(PASSES):
             nc.sync.dma_start(wf_raw[a], wf[a * 512:(a + 1) * 512, :].rearrange("(p i) r -> p i r", i=PACK))
@@ -176,7 +172,8 @@ def tile_list_tactile_contact_torque_kernel(tc, tab_words, tab_scales, offs, wf,
                 force(a, b, step)
 
         for b in range(BANKS):
-            nc.scalar.activation(share(root, b), share(mag, b), ACT.Abs_reciprocal_sqrt, bias=1.0)
+            nc.scalar.activation(share(root, b).rearrange("p (t j) -> p t j", t=PACK), mag[b // PACK][:, :, (b % PACK) * JB:(b % PACK + 1) * JB],
+                                 ACT.Abs_reciprocal_sqrt, bias=1.0)
             nc.scalar.activation(share(damp, b), share(root, b), ACT.Square)
 
         nc.vector.tensor_copy(wj_bf[:].rearrange("p (c e t) -> p c t e", e=4, t=PACK), wj_raw.rearrange("p t (c e) -> p c t e", e=4))

@@ -47,11 +47,9 @@ def tile_list_tactile_contact_torque_kernel(tc, tab_words, tab_scales, offs, wf,
         ws_w_raw = sb("ws_w_raw", [P, PASSES, H // 2], I32)
         ws_s_raw = sb("ws_s_raw", [P, H // 4], I32)
         tab_s = sb("tab_s", [P, T // 4], I32)
-        tab_first = sb("tab_first", [P, T], I32)
         picked_s = landing("picked_s", [P, S], U8, 1)
-        tab_later = landing("tab_later", [P, PASSES - 1, T], I32, 1)
-        tab_w = [tab_first[:]] + [tab_later[:, a, :] for a in range(PASSES - 1)]
-        staged = landing("staged", [P, (S + H) // 4], I32, 2)
+        tab_w = [landing("tab_w0", [P, T], I32, 2)[:], sb("tab_w1", [P, T], I32)[:], landing("tab_w2", [P, T], I32, 1)[:]]
+        staged = sb("staged", [P, (S + H) // 4], I32)
         late = landing("late", [P, PACK * (PASSES * H + N) + N_TILES], F32, 2)
         wf_raw = [late[:, a * PACK * H:(a + 1) * PACK * H].rearrange("p (i r) -> p i r", i=PACK) for a in range(PASSES)]
         wj_raw = late[:, PACK * PASSES * H:PACK * (PASSES * H + N)].rearrange("p (t n) -> p t n", t=PACK)
@@ -93,6 +91,7 @@ def tile_list_tactile_contact_torque_kernel(tc, tab_words, tab_scales, offs, wf,
             nc.sync.dma_start(rows_sb[ROW0 + 32:ROW0 + ROWS, :], rows_hbm[:, 2, :])
         nc.sync.dma_start(ws_w_raw[:], ws_words.bitcast(I32).rearrange("a p n -> p a n"))
         load_table(0)
+        load_table(1)
         nc.gpsimd.memset(warm[:, 0:1], 1.0)
         nc.scalar.activation(warm[:, 1:2], warm[:, 0:1], ACT.Abs_reciprocal_sqrt)
 
@@ -104,11 +103,10 @@ def tile_list_tactile_contact_torque_kernel(tc, tab_words, tab_scales, offs, wf,
             row = ROW0 + quad * 8
             queue = nc.scalar if quad % 2 else nc.sync
             queue.dma_start(planes_early[32 * quad:32 * quad + 4, :, :].bitcast(I32), staged[row:row + 8, :])
-        load_table(1)
+        load_table(2)
         for quad in range(4):
             row = ROW0 + 32 + quad * 4
             nc.sync.dma_start(planes_last[32 * quad:32 * quad + 4, :].bitcast(I32), staged[row:row + 4, :])
-        load_table(2)
         nc.vector.tensor_copy(ws_w[:].rearrange("p a (t g w) -> p a t g w", t=PACK, w=2),
                               ws_w_raw[:].rearrange("p a (g t w) -> p a t g w", t=PACK, w=2))
 

@@ -174,7 +174,7 @@ def tile_list_tactile_contact_torque_kernel(tc, tab_words, tab_scales, offs, wf,
                                  ACT.Abs_reciprocal_sqrt, bias=1.0)
             nc.scalar.activation(share(damp, b), share(root, b), ACT.Square)
 
-        nc.vector.tensor_copy(wj_bf[:].rearrange("p (c e t) -> p c t e", e=4, t=PACK), wj_raw.rearrange("p t (c e) -> p c t e", e=4))
+        nc.gpsimd.tensor_copy(wj_bf[:].rearrange("p (n t) -> p n t", t=PACK), wj_raw.rearrange("p t n -> p n t"))
 
         def multiply(b):
             nc.vector.tensor_tensor(share(h_bf, b).rearrange("p (c e t) -> p c t e", e=2, t=PACK),

@@ -74,11 +74,11 @@ def tile_list_tactile_contact_torque_kernel(tc, tab_words, tab_scales, offs, wf,
         banks = [psum.tile([P, PACK * JB], F32, name="bank%d" % b) for b in range(BANKS)]
 
         nc.vector.memset(tab_s[0:ROW0, :], 0)
-        nc.gpsimd.memset(tab_s[ROW0 + ROWS:P, :], 0)
+        nc.vector.memset(tab_s[ROW0 + ROWS:P, :], 0)
         for rows in (slice(0, ROW0), slice(ROW0 + ROWS, P)):
-            nc.gpsimd.memset(ws_s_raw[rows, :], 0)
+            nc.vector.memset(ws_s_raw[rows, :], 0)
         nc.vector.memset(planes_early[:].bitcast(I32), 0)
-        nc.gpsimd.memset(planes_last[:].bitcast(I32), 0)
+        nc.vector.memset(planes_last[:].bitcast(I32), 0)
 
         def load_table(a):
             nc.sync.dma_start(tab_w[a], tab_words[a].rearrange("p t i -> p (t i)").bitcast(I32))
@@ -92,7 +92,7 @@ def tile_list_tactile_contact_torque_kernel(tc, tab_words, tab_scales, offs, wf,
         nc.sync.dma_start(ws_w_raw[:], ws_words.bitcast(I32).rearrange("a p n -> p a n"))
         load_table(0)
         load_table(1)
-        nc.gpsimd.memset(warm[:, 0:1], 1.0)
+        nc.vector.memset(warm[:, 0:1], 1.0)
         nc.scalar.activation(warm[:, 1:2], warm[:, 0:1], ACT.Abs_reciprocal_sqrt)
 
         nc.vector.tensor_copy(picked_s[:], tab_s[:].bitcast(U8).indirect(offsets[:]))
@@ -165,9 +165,12 @@ def tile_list_tactile_contact_torque_kernel(tc, tab_words, tab_scales, offs, wf,
             cast_wf(a, 1)
             quant_wf(a, 0)
             quant_wf(a, 1)
-        for b in range(BANKS):
+        def force_block(b):
             for step, a in enumerate((0, 1, 2) if b < BANKS // 2 else (0, 2, 1)):
                 force(a, b, step)
+
+        for b in range(BANKS // 2):
+            force_block(b)
 
         for b in range(BANKS):
             nc.scalar.activation(share(root, b).rearrange("p (t j) -> p t j", t=PACK), mag[b // PACK][:, :, (b % PACK) * JB:(b % PACK + 1) * JB],
@@ -189,10 +192,12 @@ def tile_list_tactile_contact_torque_kernel(tc, tab_words, tab_scales, offs, wf,
         def place(c, n):
             first, count = CHUNKS[c]
             w = widths[c]
+            if c == 1:
+                return banks[(1, 0, 0)[n]][:, (1, 0, 1)[n] * w:((1, 0, 1)[n] + 1) * w]
             if count == 2:
                 return banks[first + n // 2][:, (n % 2) * w:(n % 2 + 1) * w]
             if c == last and n == 2:
-                return banks[1][:, 2 * JB:3 * JB]
+                return banks[2][:, 0:w]
             return banks[first][:, n * w:(n + 1) * w]
 
         def finish(c):
@@ -201,11 +206,14 @@ def tile_list_tactile_contact_torque_kernel(tc, tab_words, tab_scales, offs, wf,
                 nc.tensor.matmul_mx(out=place(c, n), lhsT=wj_w[:, n * P:(n + 1) * P].bitcast(FP8X4), lhsT_scale=wj_s[:, n * P:(n + 1) * P],
                                     rhs=h_w[c][:].bitcast(FP8X4), rhs_scale=h_s[c][:], start=True, stop=True)
             for n in range(N_TILES):
-                if c == 0 or (c == last and n == 2):
+                if c in (0, last - 1) or (c == last and n == 2):
                     nc.vector.tensor_scalar(res[c][:, n, :], place(c, n), bias[:, n:n + 1], None, ALU.add)
                 else:
                     nc.scalar.activation(res[c][:, n, :], place(c, n), ACT.Identity, bias=bias[:, n:n + 1])
-            nc.sync.dma_start(out.rearrange("(n p) j -> p n j", p=P)[:, :, j0:j0 + widths[c]], res[c][:])
+                if c in (1, 2):
+                    nc.sync.dma_start(out[n * P:(n + 1) * P, j0:j0 + widths[c]], res[c][:, n, :])
+            if c not in (1, 2):
+                nc.sync.dma_start(out.rearrange("(n p) j -> p n j", p=P)[:, :, j0:j0 + widths[c]], res[c][:])
 
         nc.vector.quantize_mx(out=wj_w[:, 0:256].bitcast(FP8X4), scales=wj_s[:, 0:256], in_=wj_bf[:, 0:1024])
         nc.vector.quantize_mx(out=wj_w[:, 256:384].bitcast(FP8X4), scales=wj_s[:, 256:384], in_=wj_bf[:, 1024:1536])
@@ -213,4 +221,10 @@ def tile_list_tactile_contact_torque_kernel(tc, tab_words, tab_scales, offs, wf,
             for b in range(first, first + count):
                 multiply(b)
             quant_h(c)
-            finish(c)
+            if c == last:
+                finish(c - 1)
+            if c != last - 1:
+                finish(c)
+            if c < 2:
+                force_block(BANKS // 2 + 2 * c)
+                force_block(BANKS // 2 + 2 * c + 1)

@@ -25,6 +25,7 @@ CHUNKS = ((0, 2), (2, 2), (4, 2), (6, 1), (7, 1))
 N_TILES = N // P
 ROWS = 16 * PASSES
 ROW0 = 48
+TWICE = 3
 
 
 def tile_list_tactile_contact_torque_kernel(tc, tab_words, tab_scales, offs, wf, ws_words, ws_scales, wj, bj, out):
@@ -175,14 +176,19 @@ def tile_list_tactile_contact_torque_kernel(tc, tab_words, tab_scales, offs, wf,
         for b in range(BANKS):
             nc.scalar.activation(share(root, b).rearrange("p (t j) -> p t j", t=PACK), mag[b // PACK][:, :, (b % PACK) * JB:(b % PACK + 1) * JB],
                                  ACT.Abs_reciprocal_sqrt, bias=1.0)
-            nc.scalar.activation(share(damp, b), share(root, b), ACT.Square)
+            if b != TWICE:
+                nc.scalar.activation(share(damp, b), share(root, b), ACT.Square)
 
         nc.gpsimd.tensor_copy(wj_bf[:].rearrange("p (n t) -> p n t", t=PACK), wj_raw.rearrange("p t n -> p n t"))
 
         def multiply(b):
+            left, right = banks[b][:], share(damp, b)
+            if b == TWICE:
+                nc.vector.tensor_tensor(share(damp, b), banks[b][:], share(root, b), ALU.mult)
+                left, right = share(damp, b), share(root, b)
             nc.vector.tensor_tensor(share(h_bf, b).rearrange("p (c e t) -> p c t e", e=2, t=PACK),
-                                    banks[b][:].rearrange("p (t c e) -> p c t e", e=2, t=PACK),
-                                    share(damp, b).rearrange("p (t c e) -> p c t e", e=2, t=PACK), ALU.mult)
+                                    left.rearrange("p (t c e) -> p c t e", e=2, t=PACK),
+                                    right.rearrange("p (t c e) -> p c t e", e=2, t=PACK), ALU.mult)
 
         def quant_h(c):
             nc.vector.quantize_mx(out=h_w[c][:].bitcast(FP8X4), scales=h_s[c][:], in_=h_bf[c][:])
@@ -192,12 +198,14 @@ def tile_list_tactile_contact_torque_kernel(tc, tab_words, tab_scales, offs, wf,
         def place(c, n):
             first, count = CHUNKS[c]
             w = widths[c]
+            if c == 0:
+                return banks[(0, 1, 1)[n]][:, (0, 0, 1)[n] * w:((0, 0, 1)[n] + 1) * w]
             if c == 1:
-                return banks[(1, 0, 0)[n]][:, (1, 0, 1)[n] * w:((1, 0, 1)[n] + 1) * w]
+                return banks[(0, 2, 2)[n]][:, (1, 0, 1)[n] * w:((1, 0, 1)[n] + 1) * w]
             if count == 2:
                 return banks[first + n // 2][:, (n % 2) * w:(n % 2 + 1) * w]
             if c == last and n == 2:
-                return banks[2][:, 0:w]
+                return banks[3][:, 0:w]
             return banks[first][:, n * w:(n + 1) * w]
 
         def finish(c):
@@ -206,13 +214,13 @@ def tile_list_tactile_contact_torque_kernel(tc, tab_words, tab_scales, offs, wf,
                 nc.tensor.matmul_mx(out=place(c, n), lhsT=wj_w[:, n * P:(n + 1) * P].bitcast(FP8X4), lhsT_scale=wj_s[:, n * P:(n + 1) * P],
                                     rhs=h_w[c][:].bitcast(FP8X4), rhs_scale=h_s[c][:], start=True, stop=True)
             for n in range(N_TILES):
-                if c in (0, last - 1) or (c == last and n == 2):
+                if (c == 0 and n < 2) or c == last - 1 or (c == last and n == 2):
                     nc.vector.tensor_scalar(res[c][:, n, :], place(c, n), bias[:, n:n + 1], None, ALU.add)
                 else:
                     nc.scalar.activation(res[c][:, n, :], place(c, n), ACT.Identity, bias=bias[:, n:n + 1])
-                if c in (1, 2):
+                if c < 3:
                     nc.sync.dma_start(out[n * P:(n + 1) * P, j0:j0 + widths[c]], res[c][:, n, :])
-            if c not in (1, 2):
+            if c >= 3:
                 nc.sync.dma_start(out.rearrange("(n p) j -> p n j", p=P)[:, :, j0:j0 + widths[c]], res[c][:])
 
         nc.vector.quantize_mx(out=wj_w[:, 0:256].bitcast(FP8X4), scales=wj_s[:, 0:256], in_=wj_bf[:, 0:1024])

@@ -65,7 +65,8 @@ def tile_list_tactile_contact_torque_kernel(tc, tab_words, tab_scales, offs, wf,
         wj_s = sb("wj_s", [P, N], U8)
         warm = sb("warm", [P, 2], F32)
         widths = [count * JB for first, count in CHUNKS]
-        mag = [sb("mag%d" % half, [P, PACK, 512], F32) for half in range(2)]
+        mags = sb("mags", [P, PACK + 1, 512], F32)
+        mag = [mags[:, 1 - half:PACK + 1 - half, :] for half in range(2)]
         root = [sb("root%d" % c, [P, w * PACK], F32) for c, w in enumerate(widths)]
         damp = [sb("damp%d" % c, [P, w * PACK], F32) for c, w in enumerate(widths)]
         h_bf = [sb("h_bf%d" % c, [P, w * PACK], BF16) for c, w in enumerate(widths)]
@@ -141,8 +142,11 @@ def tile_list_tactile_contact_torque_kernel(tc, tab_words, tab_scales, offs, wf,
             for half in range(2):
                 gather_words(a, half * 512, (half + 1) * 512)
                 stiff(a, half)
-        for b in range(BANKS):
-            nc.scalar.activation(mag[b // PACK][:, b % PACK, :], banks[b][:], ACT.Abs)
+        def magnitudes(first, end):
+            for b in range(first, end):
+                nc.scalar.activation(mag[b // PACK][:, b % PACK, :], banks[b][:], ACT.Abs)
+
+        magnitudes(0, PACK + 1)
 
         for a in range(PASSES):
             nc.sync.dma_start(wf_raw[a], wf[a * 512:(a + 1) * 512, :].rearrange("(p i) r -> p i r", i=PACK))
@@ -167,13 +171,15 @@ def tile_list_tactile_contact_torque_kernel(tc, tab_words, tab_scales, offs, wf,
             quant_wf(a, 0)
             quant_wf(a, 1)
         def force_block(b):
-            for step, a in enumerate((0, 1, 2) if b < BANKS // 2 else (0, 2, 1)):
+            for step, a in enumerate((0, 1, 2) if b < BANKS // 2 else (2, 0, 1)):
                 force(a, b, step)
 
         for b in range(BANKS // 2):
             force_block(b)
 
         for b in range(BANKS):
+            if b == PACK:
+                magnitudes(PACK + 1, BANKS)
             nc.scalar.activation(share(root, b).rearrange("p (t j) -> p t j", t=PACK), mag[b // PACK][:, :, (b % PACK) * JB:(b % PACK + 1) * JB],
                                  ACT.Abs_reciprocal_sqrt, bias=1.0)
             if b != TWICE:
@@ -214,7 +220,7 @@ def tile_list_tactile_contact_torque_kernel(tc, tab_words, tab_scales, offs, wf,
                 nc.tensor.matmul_mx(out=place(c, n), lhsT=wj_w[:, n * P:(n + 1) * P].bitcast(FP8X4), lhsT_scale=wj_s[:, n * P:(n + 1) * P],
                                     rhs=h_w[c][:].bitcast(FP8X4), rhs_scale=h_s[c][:], start=True, stop=True)
             for n in range(N_TILES):
-                if (c == 0 and n < 2) or c == last - 1 or (c == last and n == 2):
+                if c == 0 or c == last - 1 or (c == last and n == 2):
                     nc.vector.tensor_scalar(res[c][:, n, :], place(c, n), bias[:, n:n + 1], None, ALU.add)
                 else:
                     nc.scalar.activation(res[c][:, n, :], place(c, n), ACT.Identity, bias=bias[:, n:n + 1])

@@ -25,7 +25,7 @@ CHUNKS = ((0, 2), (2, 2), (4, 2), (6, 1), (7, 1))
 N_TILES = N // P
 ROWS = 16 * PASSES
 ROW0 = 48
-TWICE = 3
+ON_VECTOR = 1
 
 
 def tile_list_tactile_contact_torque_kernel(tc, tab_words, tab_scales, offs, wf, ws_words, ws_scales, wj, bj, out):
@@ -57,18 +57,18 @@ def tile_list_tactile_contact_torque_kernel(tc, tab_words, tab_scales, offs, wf,
         bias = late[:, PACK * (PASSES * H + N):PACK * (PASSES * H + N) + N_TILES]
         v_w = [sb("v_w%d" % a, [P, S], U32) for a in range(PASSES)]
         ws_w = sb("ws_w", [P, PASSES, H // 2], I32)
-        wf_bf = [sb("wf_bf%d" % a, [P, H * PACK], BF16) for a in range(PASSES)]
+        wf_bf = [landing("wf_bf%d" % a, [P, H * PACK], BF16, 3 + a) for a in range(PASSES)]
         wf_w = [sb("wf_w%d" % a, [P, H], U32) for a in range(PASSES)]
         wf_s = [sb("wf_s%d" % a, [P, H], U8) for a in range(PASSES)]
-        wj_bf = sb("wj_bf", [P, N * PACK], BF16)
         wj_w = sb("wj_w", [P, N], U32)
         wj_s = sb("wj_s", [P, N], U8)
         warm = sb("warm", [P, 2], F32)
         widths = [count * JB for first, count in CHUNKS]
         mags = sb("mags", [P, PACK + 1, 512], F32)
         mag = [mags[:, 1 - half:PACK + 1 - half, :] for half in range(2)]
-        root = [sb("root%d" % c, [P, w * PACK], F32) for c, w in enumerate(widths)]
-        damp = [sb("damp%d" % c, [P, w * PACK], F32) for c, w in enumerate(widths)]
+        root = [landing("root%d" % b, [P, 512], F32, 10 + b) for b in range(BANKS)]
+        damp = [landing("damp%d" % b, [P, 512], F32, 5 if b == ON_VECTOR else 20 + b) for b in range(BANKS)]
+        wj_bf = landing("wj_bf", [P, N * PACK], BF16, 10 + ON_VECTOR)
         h_bf = [sb("h_bf%d" % c, [P, w * PACK], BF16) for c, w in enumerate(widths)]
         h_w = [sb("h_w%d" % c, [P, w], U32) for c, w in enumerate(widths)]
         h_s = [sb("h_s%d" % c, [P, w], U8) for c, w in enumerate(widths)]
@@ -171,27 +171,25 @@ def tile_list_tactile_contact_torque_kernel(tc, tab_words, tab_scales, offs, wf,
             quant_wf(a, 0)
             quant_wf(a, 1)
         def force_block(b):
-            for step, a in enumerate((0, 1, 2) if b < BANKS // 2 else (2, 0, 1)):
+            for step, a in enumerate((0, 1, 2) if b <= BANKS // 2 else (2, 0, 1)):
                 force(a, b, step)
 
         for b in range(BANKS // 2):
             force_block(b)
 
         for b in range(BANKS):
-            if b == PACK:
-                magnitudes(PACK + 1, BANKS)
-            nc.scalar.activation(share(root, b).rearrange("p (t j) -> p t j", t=PACK), mag[b // PACK][:, :, (b % PACK) * JB:(b % PACK + 1) * JB],
+            nc.scalar.activation(root[b][:].rearrange("p (t j) -> p t j", t=PACK), mag[b // PACK][:, :, (b % PACK) * JB:(b % PACK + 1) * JB],
                                  ACT.Abs_reciprocal_sqrt, bias=1.0)
-            if b != TWICE:
-                nc.scalar.activation(share(damp, b), share(root, b), ACT.Square)
+            if b == PACK - 1:
+                magnitudes(PACK + 1, BANKS)
+            if b != ON_VECTOR:
+                nc.scalar.activation(damp[b][:], root[b][:], ACT.Square)
 
+        nc.vector.tensor_tensor(damp[ON_VECTOR][:], root[ON_VECTOR][:], root[ON_VECTOR][:], ALU.mult)
         nc.gpsimd.tensor_copy(wj_bf[:].rearrange("p (n t) -> p n t", t=PACK), wj_raw.rearrange("p t n -> p n t"))
 
         def multiply(b):
-            left, right = banks[b][:], share(damp, b)
-            if b == TWICE:
-                nc.vector.tensor_tensor(share(damp, b), banks[b][:], share(root, b), ALU.mult)
-                left, right = share(damp, b), share(root, b)
+            left, right = banks[b][:], damp[b][:]
             nc.vector.tensor_tensor(share(h_bf, b).rearrange("p (c e t) -> p c t e", e=2, t=PACK),
                                     left.rearrange("p (t c e) -> p c t e", e=2, t=PACK),
                                     right.rearrange("p (t c e) -> p c t e", e=2, t=PACK), ALU.mult)

@@ -32,6 +32,7 @@ def tile_list_tactile_contact_torque_kernel(tc, tab_words, tab_scales, offs, wf,
     nc = tc.nc
     with ExitStack() as ctx:
         keep = ctx.enter_context(tc.tile_pool(name="keep", bufs=1))
+        laid = ctx.enter_context(tc.tile_pool(name="laid", bufs=1))
         psum = ctx.enter_context(tc.psum_pool(name="psum", bufs=1))
 
         def sb(name, shape, dtype):
@@ -67,10 +68,12 @@ def tile_list_tactile_contact_torque_kernel(tc, tab_words, tab_scales, offs, wf,
         mags = sb("mags", [P, PACK + 1, 512], F32)
         mag = [mags[:, 1 - half:PACK + 1 - half, :] for half in range(2)]
         root = [landing("root%d" % b, [P, 512], F32, 10 + b) for b in range(BANKS)]
-        damp = [landing("damp%d" % b, [P, 512], F32, 5 if b == ON_VECTOR else 20 + b) for b in range(BANKS)]
-        wj_bf = landing("wj_bf", [P, N * PACK], BF16, 10 + ON_VECTOR)
+        damp = [laid.tile([P, 512], F32, name="damp3", align_bytes=64, offset=0) if b == 3
+                else landing("damp%d" % b, [P, 512], F32, 5 if b == ON_VECTOR else 20 + b) for b in range(BANKS)]
+        wj_bf = landing("wj_bf", [P, 2 * P * PACK], BF16, 10 + ON_VECTOR)
+        wj_bf_third = laid.tile([P, P * PACK], BF16, name="wj_bf_third", align_bytes=64, offset=0)
         h_bf = [sb("h_bf%d" % c, [P, w * PACK], BF16) for c, w in enumerate(widths)]
-        h_w = [sb("h_w%d" % c, [P, w], U32) for c, w in enumerate(widths)]
+        h_w = [sb("h_w%d" % c, [P, w], U32) if c else laid.tile([P, w], U32, name="h_w0", align_bytes=64, offset=1024) for c, w in enumerate(widths)]
         h_s = [sb("h_s%d" % c, [P, w], U8) for c, w in enumerate(widths)]
         res = [sb("res%d" % c, [P, N_TILES, w], F32) for c, w in enumerate(widths)]
         banks = [psum.tile([P, PACK * JB], F32, name="bank%d" % b) for b in range(BANKS)]
@@ -186,7 +189,8 @@ def tile_list_tactile_contact_torque_kernel(tc, tab_words, tab_scales, offs, wf,
                 nc.scalar.activation(damp[b][:], root[b][:], ACT.Square)
 
         nc.vector.tensor_tensor(damp[ON_VECTOR][:], root[ON_VECTOR][:], root[ON_VECTOR][:], ALU.mult)
-        nc.gpsimd.tensor_copy(wj_bf[:].rearrange("p (n t) -> p n t", t=PACK), wj_raw.rearrange("p t n -> p n t"))
+        nc.gpsimd.tensor_scalar(wj_bf[:].rearrange("p (n t) -> p n t", t=PACK), wj_raw[:, :, 0:2 * P].rearrange("p t n -> p n t"),
+                                1.0, 0.0, ALU.mult, ALU.add)
 
         def multiply(b):
             left, right = banks[b][:], damp[b][:]
@@ -227,16 +231,25 @@ def tile_list_tactile_contact_torque_kernel(tc, tab_words, tab_scales, offs, wf,
             if c >= 3:
                 nc.sync.dma_start(out.rearrange("(n p) j -> p n j", p=P)[:, :, j0:j0 + widths[c]], res[c][:])
 
-        nc.vector.quantize_mx(out=wj_w[:, 0:256].bitcast(FP8X4), scales=wj_s[:, 0:256], in_=wj_bf[:, 0:1024])
-        nc.vector.quantize_mx(out=wj_w[:, 256:384].bitcast(FP8X4), scales=wj_s[:, 256:384], in_=wj_bf[:, 1024:1536])
-        for c, (first, count) in enumerate(CHUNKS):
-            for b in range(first, first + count):
-                multiply(b)
+        for b in range(PACK):
+            multiply(b)
+        quant_h(0)
+        nc.vector.tensor_copy(wj_bf_third[:].rearrange("p (g e t) -> p g t e", e=4, t=PACK),
+                              wj_raw[:, :, 2 * P:].rearrange("p t (g e) -> p g t e", e=4))
+        nc.vector.quantize_mx(out=wj_w[:, 0:256].bitcast(FP8X4), scales=wj_s[:, 0:256], in_=wj_bf[:])
+        nc.vector.quantize_mx(out=wj_w[:, 256:384].bitcast(FP8X4), scales=wj_s[:, 256:384], in_=wj_bf_third[:])
+        finish(0)
+        force_block(4)
+        force_block(5)
+        for c, (first, count) in list(enumerate(CHUNKS))[1:]:
+            if c > 1:
+                for b in range(first, first + count):
+                    multiply(b)
             quant_h(c)
             if c == last:
                 finish(c - 1)
             if c != last - 1:
                 finish(c)
-            if c < 2:
-                force_block(BANKS // 2 + 2 * c)
-                force_block(BANKS // 2 + 2 * c + 1)
+            if c == 1:
+                force_block(6)
+                force_block(7)

@@ -19,13 +19,16 @@ ALU = mybir.AluOpType
 P = 128
 PACK = 4
 PASSES = K // (P * PACK)
-BANKS = 8
-JB = S // BANKS
+BLOCKS = 8
+JB = S // BLOCKS
+JQ = 2 * JB
+QUARTERS = S // JQ
 CHUNKS = ((0, 2), (2, 2), (4, 2), (6, 1), (7, 1))
 N_TILES = N // P
 ROWS = 16 * PASSES
 ROW0 = 48
 ON_VECTOR = 1
+BESIDE_CAST = 5
 
 
 def tile_list_tactile_contact_torque_kernel(tc, tab_words, tab_scales, offs, wf, ws_words, ws_scales, wj, bj, out):
@@ -35,58 +38,56 @@ def tile_list_tactile_contact_torque_kernel(tc, tab_words, tab_scales, offs, wf,
         laid = ctx.enter_context(tc.tile_pool(name="laid", bufs=1))
         psum = ctx.enter_context(tc.psum_pool(name="psum", bufs=1))
 
-        def sb(name, shape, dtype):
-            return keep.tile(shape, dtype, name=name, align_bytes=64)
+        def sb(name, shape, dtype, slot=None):
+            return keep.tile(shape, dtype, name=name, tag=slot or name, align_bytes=64)
+
+        def at(name, shape, dtype, offset):
+            return laid.tile(shape, dtype, name=name, align_bytes=64, offset=offset)
 
         offsets = keep.tile([P, S // 16], U16, name="offsets")
         planes_early = sb("planes_early", [P, 2, S + H], U8)
+        ws_w_raw = sb("ws_w_raw", [P, PASSES, H // 2], I32)
         planes_last = sb("planes_last", [P, S + H], U8)
         planes = [planes_early[:, 0, :], planes_early[:, 1, :], planes_last[:]]
-
-        def landing(name, shape, dtype, slot):
-            return keep.tile(shape, dtype, name=name, tag="landing%d" % slot, align_bytes=64)
-
-        ws_w_raw = sb("ws_w_raw", [P, PASSES, H // 2], I32)
         ws_s_raw = sb("ws_s_raw", [P, H // 4], I32)
         tab_s = sb("tab_s", [P, T // 4], I32)
-        picked_s = landing("picked_s", [P, S], U8, 1)
-        tab_w = [landing("tab_w0", [P, T], I32, 2)[:], sb("tab_w1", [P, T], I32)[:], landing("tab_w2", [P, T], I32, 1)[:]]
+        picked_s = at("picked_s", [P, S], U8, 4 * T - S // 2)
+        ws_w = sb("ws_w", [P, PASSES, H // 2], I32)
+        tab_w = [sb("tab_w0", [P, T], I32, "tab0"), at("tab_w1", [P, T], I32, 0), at("tab_w2", [P, T], I32, 4 * T)]
         staged = sb("staged", [P, (S + H) // 4], I32)
-        late = landing("late", [P, PACK * (PASSES * H + N) + N_TILES], F32, 2)
+        late = sb("late", [P, PACK * (PASSES * H + N) + N_TILES], F32, "tab0")
         wf_raw = [late[:, a * PACK * H:(a + 1) * PACK * H].rearrange("p (i r) -> p i r", i=PACK) for a in range(PASSES)]
         wj_raw = late[:, PACK * PASSES * H:PACK * (PASSES * H + N)].rearrange("p (t n) -> p t n", t=PACK)
         bias = late[:, PACK * (PASSES * H + N):PACK * (PASSES * H + N) + N_TILES]
         v_w = [sb("v_w%d" % a, [P, S], U32) for a in range(PASSES)]
-        ws_w = sb("ws_w", [P, PASSES, H // 2], I32)
-        wf_bf = [landing("wf_bf%d" % a, [P, H * PACK], BF16, 3 + a) for a in range(PASSES)]
+        wf_bf = [sb("wf_bf%d" % a, [P, H * PACK], BF16) for a in range(PASSES)]
         wf_w = [sb("wf_w%d" % a, [P, H], U32) for a in range(PASSES)]
         wf_s = [sb("wf_s%d" % a, [P, H], U8) for a in range(PASSES)]
         wj_w = sb("wj_w", [P, N], U32)
         wj_s = sb("wj_s", [P, N], U8)
         warm = sb("warm", [P, 2], F32)
         widths = [count * JB for first, count in CHUNKS]
-        mags = sb("mags", [P, PACK + 1, 512], F32)
-        mag = [mags[:, 1 - half:PACK + 1 - half, :] for half in range(2)]
-        root = [landing("root%d" % b, [P, 512], F32, 10 + b) for b in range(BANKS)]
-        damp = [laid.tile([P, 512], F32, name="damp3", align_bytes=64, offset=0) if b == 3
-                else landing("damp%d" % b, [P, 512], F32, 5 if b == ON_VECTOR else 20 + b) for b in range(BANKS)]
-        wj_bf = landing("wj_bf", [P, 2 * P * PACK], BF16, 10 + ON_VECTOR)
-        wj_bf_third = laid.tile([P, P * PACK], BF16, name="wj_bf_third", align_bytes=64, offset=0)
+        mag = [sb("mag%d" % q, [P, PACK, JQ], F32) for q in range(QUARTERS)]
+        root = [sb("root%d" % b, [P, PACK * JB], F32) for b in range(BLOCKS)]
+        spare = 8 * T
+        damp = [at("damp4", [P, PACK * JB], F32, spare) if b == BESIDE_CAST - 1
+                else sb("damp%d" % b, [P, PACK * JB], F32, "wf_bf2" if b == ON_VECTOR else None) for b in range(BLOCKS)]
+        wj_bf = sb("wj_bf", [P, N * PACK], BF16, "root%d" % ON_VECTOR)
         h_bf = [sb("h_bf%d" % c, [P, w * PACK], BF16) for c, w in enumerate(widths)]
-        h_w = [sb("h_w%d" % c, [P, w], U32) if c else laid.tile([P, w], U32, name="h_w0", align_bytes=64, offset=1024) for c, w in enumerate(widths)]
+        h_w = [sb("h_w%d" % c, [P, w], U32) if c else at("h_w0", [P, w], U32, spare + 1024) for c, w in enumerate(widths)]
         h_s = [sb("h_s%d" % c, [P, w], U8) for c, w in enumerate(widths)]
         res = [sb("res%d" % c, [P, N_TILES, w], F32) for c, w in enumerate(widths)]
-        banks = [psum.tile([P, PACK * JB], F32, name="bank%d" % b) for b in range(BANKS)]
+        banks = [psum.tile([P, PACK * JB], F32, name="bank%d" % b) for b in range(BLOCKS)]
 
         nc.vector.memset(tab_s[0:ROW0, :], 0)
-        nc.vector.memset(tab_s[ROW0 + ROWS:P, :], 0)
-        for rows in (slice(0, ROW0), slice(ROW0 + ROWS, P)):
-            nc.vector.memset(ws_s_raw[rows, :], 0)
+        nc.gpsimd.memset(tab_s[ROW0 + ROWS:P, :], 0)
+        nc.vector.memset(ws_s_raw[0:ROW0, :], 0)
+        nc.vector.memset(ws_s_raw[ROW0 + ROWS:P, :], 0)
         nc.vector.memset(planes_early[:].bitcast(I32), 0)
         nc.vector.memset(planes_last[:].bitcast(I32), 0)
 
         def load_table(a):
-            nc.sync.dma_start(tab_w[a], tab_words[a].rearrange("p t i -> p (t i)").bitcast(I32))
+            nc.sync.dma_start(tab_w[a][:], tab_words[a].rearrange("p t i -> p (t i)").bitcast(I32))
 
         nc.sync.dma_start(offsets[:], offs)
         ws_scales_i = ws_scales.bitcast(I32).rearrange("a q n -> q a n")
@@ -96,7 +97,6 @@ def tile_list_tactile_contact_torque_kernel(tc, tab_words, tab_scales, offs, wf,
             nc.sync.dma_start(rows_sb[ROW0 + 32:ROW0 + ROWS, :], rows_hbm[:, 2, :])
         nc.sync.dma_start(ws_w_raw[:], ws_words.bitcast(I32).rearrange("a p n -> p a n"))
         load_table(0)
-        load_table(1)
         nc.vector.memset(warm[:, 0:1], 1.0)
         nc.scalar.activation(warm[:, 1:2], warm[:, 0:1], ACT.Abs_reciprocal_sqrt)
 
@@ -108,48 +108,36 @@ def tile_list_tactile_contact_torque_kernel(tc, tab_words, tab_scales, offs, wf,
             row = ROW0 + quad * 8
             queue = nc.scalar if quad % 2 else nc.sync
             queue.dma_start(planes_early[32 * quad:32 * quad + 4, :, :].bitcast(I32), staged[row:row + 8, :])
+        load_table(1)
         load_table(2)
         for quad in range(4):
             row = ROW0 + 32 + quad * 4
             nc.sync.dma_start(planes_last[32 * quad:32 * quad + 4, :].bitcast(I32), staged[row:row + 4, :])
+
         nc.vector.tensor_copy(ws_w[:].rearrange("p a (t g w) -> p a t g w", t=PACK, w=2),
                               ws_w_raw[:].rearrange("p a (g t w) -> p a t g w", t=PACK, w=2))
 
         def gather_words(a, j0, j1):
-            nc.vector.tensor_copy(v_w[a][:, j0:j1], tab_w[a].bitcast(U32).indirect(offsets[:, j0 // 16:j1 // 16]))
+            nc.vector.tensor_copy(v_w[a][:, j0:j1], tab_w[a][:].bitcast(U32).indirect(offsets[:, j0 // 16:j1 // 16]))
 
-        def stiff(a, half):
-            cols = slice(half * 512, (half + 1) * 512)
+        def stiff(a, q):
+            cols = slice(q * JQ, (q + 1) * JQ)
             for t in range(PACK):
                 nc.tensor.matmul_mx(
-                    out=banks[PACK * half + t][:], lhsT=ws_w[:, a, t * 64:(t + 1) * 64].bitcast(FP4X4),
+                    out=banks[2 * q + t // 2][:, (t % 2) * JQ:(t % 2 + 1) * JQ], lhsT=ws_w[:, a, t * 64:(t + 1) * 64].bitcast(FP4X4),
                     lhsT_scale=planes[a][:, S + t * P:S + (t + 1) * P],
                     rhs=v_w[a][:, cols].bitcast(FP8X4), rhs_scale=planes[a][:, cols],
-                    start=(a == 0), stop=(a == PASSES - 1))
-
-        def force(a, b, step):
-            cols = slice(b * JB, (b + 1) * JB)
-            for t in range(PACK):
-                nc.tensor.matmul_mx(
-                    out=banks[b][:, t * JB:(t + 1) * JB], lhsT=wf_w[a][:, t * P:(t + 1) * P].bitcast(FP8X4),
-                    lhsT_scale=wf_s[a][:, t * P:(t + 1) * P],
-                    rhs=v_w[a][:, cols].bitcast(FP8X4), rhs_scale=planes[a][:, cols],
-                    start=(step == 0 and t == 0), stop=(step == PASSES - 1 and t == PACK - 1))
-
-        def share(tiles, b):
-            c = max(i for i, (first, count) in enumerate(CHUNKS) if first <= b)
-            o = (b - CHUNKS[c][0]) * 512
-            return tiles[c][:, o:o + 512]
+                    start=(a == 0 and t % 2 == 0), stop=(a == PASSES - 1 and t % 2 == 1))
 
         for a in range(PASSES):
-            for half in range(2):
-                gather_words(a, half * 512, (half + 1) * 512)
-                stiff(a, half)
-        def magnitudes(first, end):
-            for b in range(first, end):
-                nc.scalar.activation(mag[b // PACK][:, b % PACK, :], banks[b][:], ACT.Abs)
+            step = 1 if a == PASSES - 1 else 2
+            for q in range(0, QUARTERS, step):
+                gather_words(a, q * JQ, (q + step) * JQ)
+                for each in range(q, q + step):
+                    stiff(a, each)
 
-        magnitudes(0, PACK + 1)
+        for b in range(BLOCKS):
+            nc.scalar.activation(mag[b // 2][:, 2 * (b % 2):2 * (b % 2) + 2, :].rearrange("p t j -> p (t j)"), banks[b][:], ACT.Abs)
 
         for a in range(PASSES):
             nc.sync.dma_start(wf_raw[a], wf[a * 512:(a + 1) * 512, :].rearrange("(p i) r -> p i r", i=PACK))
@@ -173,30 +161,36 @@ def tile_list_tactile_contact_torque_kernel(tc, tab_words, tab_scales, offs, wf,
             cast_wf(a, 1)
             quant_wf(a, 0)
             quant_wf(a, 1)
-        def force_block(b):
-            for step, a in enumerate((0, 1, 2) if b <= BANKS // 2 else (2, 0, 1)):
-                force(a, b, step)
 
-        for b in range(BANKS // 2):
-            force_block(b)
+        def force(b):
+            cols = slice(b * JB, (b + 1) * JB)
+            for a in range(PASSES):
+                for t in range(PACK):
+                    nc.tensor.matmul_mx(
+                        out=banks[b][:, t * JB:(t + 1) * JB], lhsT=wf_w[a][:, t * P:(t + 1) * P].bitcast(FP8X4),
+                        lhsT_scale=wf_s[a][:, t * P:(t + 1) * P],
+                        rhs=v_w[a][:, cols].bitcast(FP8X4), rhs_scale=planes[a][:, cols],
+                        start=(a == 0 and t == 0), stop=(a == PASSES - 1 and t == PACK - 1))
 
-        for b in range(BANKS):
-            nc.scalar.activation(root[b][:].rearrange("p (t j) -> p t j", t=PACK), mag[b // PACK][:, :, (b % PACK) * JB:(b % PACK + 1) * JB],
+        for b in range(BESIDE_CAST):
+            force(b)
+
+        for b in range(BLOCKS):
+            nc.scalar.activation(root[b][:].rearrange("p (t j) -> p t j", t=PACK), mag[b // 2][:, :, (b % 2) * JB:(b % 2 + 1) * JB],
                                  ACT.Abs_reciprocal_sqrt, bias=1.0)
-            if b == PACK - 1:
-                magnitudes(PACK + 1, BANKS)
             if b != ON_VECTOR:
                 nc.scalar.activation(damp[b][:], root[b][:], ACT.Square)
 
         nc.vector.tensor_tensor(damp[ON_VECTOR][:], root[ON_VECTOR][:], root[ON_VECTOR][:], ALU.mult)
-        nc.gpsimd.tensor_scalar(wj_bf[:].rearrange("p (n t) -> p n t", t=PACK), wj_raw[:, :, 0:2 * P].rearrange("p t n -> p n t"),
+        nc.gpsimd.tensor_scalar(wj_bf[:].rearrange("p (n t) -> p n t", t=PACK), wj_raw.rearrange("p t n -> p n t"),
                                 1.0, 0.0, ALU.mult, ALU.add)
 
         def multiply(b):
-            left, right = banks[b][:], damp[b][:]
-            nc.vector.tensor_tensor(share(h_bf, b).rearrange("p (c e t) -> p c t e", e=2, t=PACK),
-                                    left.rearrange("p (t c e) -> p c t e", e=2, t=PACK),
-                                    right.rearrange("p (t c e) -> p c t e", e=2, t=PACK), ALU.mult)
+            c = max(i for i, (first, count) in enumerate(CHUNKS) if first <= b)
+            o = (b - CHUNKS[c][0]) * PACK * JB
+            nc.vector.tensor_tensor(h_bf[c][:, o:o + PACK * JB].rearrange("p (c e t) -> p c t e", e=2, t=PACK),
+                                    banks[b][:].rearrange("p (t c e) -> p c t e", e=2, t=PACK),
+                                    damp[b][:].rearrange("p (t c e) -> p c t e", e=2, t=PACK), ALU.mult)
 
         def quant_h(c):
             nc.vector.quantize_mx(out=h_w[c][:].bitcast(FP8X4), scales=h_s[c][:], in_=h_bf[c][:])
@@ -206,14 +200,8 @@ def tile_list_tactile_contact_torque_kernel(tc, tab_words, tab_scales, offs, wf,
         def place(c, n):
             first, count = CHUNKS[c]
             w = widths[c]
-            if c == 0:
-                return banks[(0, 1, 1)[n]][:, (0, 0, 1)[n] * w:((0, 0, 1)[n] + 1) * w]
-            if c == 1:
-                return banks[(0, 2, 2)[n]][:, (1, 0, 1)[n] * w:((1, 0, 1)[n] + 1) * w]
             if count == 2:
                 return banks[first + n // 2][:, (n % 2) * w:(n % 2 + 1) * w]
-            if c == last and n == 2:
-                return banks[3][:, 0:w]
             return banks[first][:, n * w:(n + 1) * w]
 
         def finish(c):
@@ -222,7 +210,7 @@ def tile_list_tactile_contact_torque_kernel(tc, tab_words, tab_scales, offs, wf,
                 nc.tensor.matmul_mx(out=place(c, n), lhsT=wj_w[:, n * P:(n + 1) * P].bitcast(FP8X4), lhsT_scale=wj_s[:, n * P:(n + 1) * P],
                                     rhs=h_w[c][:].bitcast(FP8X4), rhs_scale=h_s[c][:], start=True, stop=True)
             for n in range(N_TILES):
-                if c == 0 or c == last - 1 or (c == last and n == 2):
+                if c >= last - 1:
                     nc.vector.tensor_scalar(res[c][:, n, :], place(c, n), bias[:, n:n + 1], None, ALU.add)
                 else:
                     nc.scalar.activation(res[c][:, n, :], place(c, n), ACT.Identity, bias=bias[:, n:n + 1])
@@ -231,25 +219,20 @@ def tile_list_tactile_contact_torque_kernel(tc, tab_words, tab_scales, offs, wf,
             if c >= 3:
                 nc.sync.dma_start(out.rearrange("(n p) j -> p n j", p=P)[:, :, j0:j0 + widths[c]], res[c][:])
 
-        for b in range(PACK):
+        for b in range(BESIDE_CAST):
             multiply(b)
         quant_h(0)
-        nc.vector.tensor_copy(wj_bf_third[:].rearrange("p (g e t) -> p g t e", e=4, t=PACK),
-                              wj_raw[:, :, 2 * P:].rearrange("p t (g e) -> p g t e", e=4))
-        nc.vector.quantize_mx(out=wj_w[:, 0:256].bitcast(FP8X4), scales=wj_s[:, 0:256], in_=wj_bf[:])
-        nc.vector.quantize_mx(out=wj_w[:, 256:384].bitcast(FP8X4), scales=wj_s[:, 256:384], in_=wj_bf_third[:])
+        nc.vector.quantize_mx(out=wj_w[:].bitcast(FP8X4), scales=wj_s[:], in_=wj_bf[:])
         finish(0)
-        force_block(4)
-        force_block(5)
+        force(5)
         for c, (first, count) in list(enumerate(CHUNKS))[1:]:
-            if c > 1:
-                for b in range(first, first + count):
-                    multiply(b)
+            for b in range(max(first, BESIDE_CAST), first + count):
+                multiply(b)
             quant_h(c)
             if c == last:
                 finish(c - 1)
             if c != last - 1:
                 finish(c)
             if c == 1:
-                force_block(6)
-                force_block(7)
+                force(6)
+                force(7)

@@ -106,8 +106,7 @@ def tile_list_tactile_contact_torque_kernel(tc, tab_words, tab_scales, offs, wf,
         nc.vector.tensor_copy(staged[:, 0:S // 4], picked_s[:].bitcast(I32))
         for quad in range(4):
             row = ROW0 + quad * 8
-            queue = nc.scalar if quad % 2 else nc.sync
-            queue.dma_start(planes_early[32 * quad:32 * quad + 4, :, :].bitcast(I32), staged[row:row + 8, :])
+            nc.sync.dma_start(planes_early[32 * quad:32 * quad + 4, :, :].bitcast(I32), staged[row:row + 8, :])
         load_table(1)
         load_table(2)
         for quad in range(4):

@@ -45,10 +45,8 @@ def tile_list_tactile_contact_torque_kernel(tc, tab_words, tab_scales, offs, wf,
             return laid.tile(shape, dtype, name=name, align_bytes=64, offset=offset)
 
         offsets = keep.tile([P, S // 16], U16, name="offsets")
-        planes_early = sb("planes_early", [P, 2, S + H], U8)
         ws_w_raw = sb("ws_w_raw", [P, PASSES, H // 2], I32)
-        planes_last = sb("planes_last", [P, S + H], U8)
-        planes = [planes_early[:, 0, :], planes_early[:, 1, :], planes_last[:]]
+        planes = [sb("plane%d" % a, [P, S + H], U8) for a in range(PASSES)]
         ws_s_raw = sb("ws_s_raw", [P, H // 4], I32)
         tab_s = sb("tab_s", [P, T // 4], I32)
         picked_s = at("picked_s", [P, S], U8, 4 * T - S // 2)
@@ -83,18 +81,18 @@ def tile_list_tactile_contact_torque_kernel(tc, tab_words, tab_scales, offs, wf,
         nc.gpsimd.memset(tab_s[ROW0 + ROWS:P, :], 0)
         nc.vector.memset(ws_s_raw[0:ROW0, :], 0)
         nc.vector.memset(ws_s_raw[ROW0 + ROWS:P, :], 0)
-        nc.vector.memset(planes_early[:].bitcast(I32), 0)
-        nc.vector.memset(planes_last[:].bitcast(I32), 0)
+        for plane in planes:
+            nc.vector.memset(plane[:].bitcast(I32), 0)
 
         def load_table(a):
             nc.sync.dma_start(tab_w[a][:], tab_words[a].rearrange("p t i -> p (t i)").bitcast(I32))
 
         nc.sync.dma_start(offsets[:], offs)
-        ws_scales_i = ws_scales.bitcast(I32).rearrange("a q n -> q a n")
-        tab_scales_i = tab_scales.bitcast(I32).rearrange("a q n -> q a n")
+        ws_scales_i = ws_scales.bitcast(I32).rearrange("a q n -> (a q) n")
+        tab_scales_i = tab_scales.bitcast(I32).rearrange("a q n -> (a q) n")
         for rows_sb, rows_hbm in ((tab_s, tab_scales_i), (ws_s_raw, ws_scales_i)):
-            nc.sync.dma_start(rows_sb[ROW0:ROW0 + 32, :], rows_hbm[:, 0:2, :])
-            nc.sync.dma_start(rows_sb[ROW0 + 32:ROW0 + ROWS, :], rows_hbm[:, 2, :])
+            nc.sync.dma_start(rows_sb[ROW0:ROW0 + 32, :], rows_hbm[0:32, :])
+            nc.sync.dma_start(rows_sb[ROW0 + 32:ROW0 + ROWS, :], rows_hbm[32:ROWS, :])
         nc.sync.dma_start(ws_w_raw[:], ws_words.bitcast(I32).rearrange("a p n -> p a n"))
         load_table(0)
         nc.vector.memset(warm[:, 0:1], 1.0)
@@ -104,14 +102,14 @@ def tile_list_tactile_contact_torque_kernel(tc, tab_words, tab_scales, offs, wf,
         nc.vector.tensor_copy(staged[:, S // 4:].rearrange("p (t g) -> p t g", t=PACK),
                               ws_s_raw[:].rearrange("p (g t) -> p t g", t=PACK))
         nc.vector.tensor_copy(staged[:, 0:S // 4], picked_s[:].bitcast(I32))
-        for quad in range(4):
-            row = ROW0 + quad * 8
-            nc.sync.dma_start(planes_early[32 * quad:32 * quad + 4, :, :].bitcast(I32), staged[row:row + 8, :])
-        load_table(1)
-        load_table(2)
-        for quad in range(4):
-            row = ROW0 + 32 + quad * 4
-            nc.sync.dma_start(planes_last[32 * quad:32 * quad + 4, :].bitcast(I32), staged[row:row + 4, :])
+        for a in range(PASSES):
+            if a == PASSES - 1:
+                load_table(a)
+            for r in range(4):
+                row = ROW0 + 16 * a
+                nc.sync.dma_start(planes[a][r:P:32, :].bitcast(I32), staged[row + r:row + 16:4, :])
+            if a == 0:
+                load_table(1)
 
         nc.vector.tensor_copy(ws_w[:].rearrange("p a (t g w) -> p a t g w", t=PACK, w=2),
                               ws_w_raw[:].rearrange("p a (g t w) -> p a t g w", t=PACK, w=2))

@@ -55,6 +55,8 @@ def tile_list_tactile_contact_torque_kernel(tc, tab_words, tab_scales, offs, wf,
         staged = sb("staged", [P, (S + H) // 4], I32)
         late = sb("late", [P, PACK * (PASSES * H + N) + N_TILES], F32, "tab0")
         wf_raw = [late[:, a * PACK * H:(a + 1) * PACK * H].rearrange("p (i r) -> p i r", i=PACK) for a in range(PASSES)]
+        wf_last = [late[:, (2 * PASSES - 2 + half) * PACK * H // 2:(2 * PASSES - 1 + half) * PACK * H // 2].rearrange("p (i r) -> p i r", i=PACK)
+                   for half in range(2)]
         wj_raw = late[:, PACK * PASSES * H:PACK * (PASSES * H + N)].rearrange("p (t n) -> p t n", t=PACK)
         bias = late[:, PACK * (PASSES * H + N):PACK * (PASSES * H + N) + N_TILES]
         v_w = [sb("v_w%d" % a, [P, S], U32) for a in range(PASSES)]
@@ -86,6 +88,9 @@ def tile_list_tactile_contact_torque_kernel(tc, tab_words, tab_scales, offs, wf,
 
         def load_table(a):
             nc.sync.dma_start(tab_w[a][:], tab_words[a].rearrange("p t i -> p (t i)").bitcast(I32))
+
+        def load_wf(a, r0, r1):
+            nc.sync.dma_start(wf_raw[a][:, :, r0:r1], wf[a * 512:(a + 1) * 512, r0:r1].rearrange("(p i) r -> p i r", i=PACK))
 
         nc.sync.dma_start(offsets[:], offs)
         ws_scales_i = ws_scales.bitcast(I32).rearrange("a q n -> (a q) n")
@@ -136,8 +141,10 @@ def tile_list_tactile_contact_torque_kernel(tc, tab_words, tab_scales, offs, wf,
         for b in range(BLOCKS):
             nc.scalar.activation(mag[b // 2][:, 2 * (b % 2):2 * (b % 2) + 2, :].rearrange("p t j -> p (t j)"), banks[b][:], ACT.Abs)
 
-        for a in range(PASSES):
-            nc.sync.dma_start(wf_raw[a], wf[a * 512:(a + 1) * 512, :].rearrange("(p i) r -> p i r", i=PACK))
+        for a in range(PASSES - 1):
+            load_wf(a, 0, H)
+        for half in range(2):
+            nc.sync.dma_start(wf_last[half], wf[(PASSES - 1) * 512:, half * H // 2:(half + 1) * H // 2].rearrange("(p i) r -> p i r", i=PACK))
         wj_rows = wj.rearrange("(g t e) n -> t g e n", t=PACK, e=4)
         for t in range(PACK):
             nc.sync.dma_start(wj_raw[:, t, :], wj_rows[t])
@@ -153,11 +160,21 @@ def tile_list_tactile_contact_torque_kernel(tc, tab_words, tab_scales, offs, wf,
             nc.vector.quantize_mx(out=wf_w[a][:, u * 256:(u + 1) * 256].bitcast(FP8X4), scales=wf_s[a][:, u * 256:(u + 1) * 256],
                                   in_=wf_bf[a][:, u * 1024:(u + 1) * 1024])
 
-        for a in range(PASSES):
+        for a in range(PASSES - 1):
             cast_wf(a, 0)
             cast_wf(a, 1)
             quant_wf(a, 0)
             quant_wf(a, 1)
+        a = PASSES - 1
+        for half in range(2):
+            for u in range(2):
+                nc.vector.tensor_copy(
+                    wf_bf[a][:].rearrange("p (t g e i) -> p t g i e", t=PACK, e=4, i=PACK)[:, 2 * u:2 * u + 2, 16 * half:16 * half + 16],
+                    wf_last[half].rearrange("p i (g t e) -> p t g i e", t=PACK, e=4)[:, 2 * u:2 * u + 2])
+            for t in range(PACK):
+                c0 = t * P + half * P // 2
+                nc.vector.quantize_mx(out=wf_w[a][:, c0:c0 + P // 2].bitcast(FP8X4), scales=wf_s[a][:, c0:c0 + P // 2],
+                                      in_=wf_bf[a][:, c0 * PACK:(c0 + P // 2) * PACK])
 
         def force(b):
             cols = slice(b * JB, (b + 1) * JB)

@@ -23,12 +23,14 @@ BLOCKS = 8
 JB = S // BLOCKS
 JQ = 2 * JB
 QUARTERS = S // JQ
-CHUNKS = ((0, 2), (2, 2), (4, 2), (6, 1), (7, 1))
+CHUNKS = ((0, 2), (2, 2), (4, 2), (7, 1), (6, 1))
 N_TILES = N // P
 ROWS = 16 * PASSES
 ROW0 = 48
-ON_VECTOR = 1
-BESIDE_CAST = 5
+ON_VECTOR = (1,)
+BESIDE_CAST = 4
+ON_GPSIMD = 6
+EARLY_BLOCKS = 5
 
 
 def tile_list_tactile_contact_torque_kernel(tc, tab_words, tab_scales, offs, wf, ws_words, ws_scales, wj, bj, out):
@@ -55,8 +57,6 @@ def tile_list_tactile_contact_torque_kernel(tc, tab_words, tab_scales, offs, wf,
         staged = sb("staged", [P, (S + H) // 4], I32)
         late = sb("late", [P, PACK * (PASSES * H + N) + N_TILES], F32, "tab0")
         wf_raw = [late[:, a * PACK * H:(a + 1) * PACK * H].rearrange("p (i r) -> p i r", i=PACK) for a in range(PASSES)]
-        wf_last = [late[:, (2 * PASSES - 2 + half) * PACK * H // 2:(2 * PASSES - 1 + half) * PACK * H // 2].rearrange("p (i r) -> p i r", i=PACK)
-                   for half in range(2)]
         wj_raw = late[:, PACK * PASSES * H:PACK * (PASSES * H + N)].rearrange("p (t n) -> p t n", t=PACK)
         bias = late[:, PACK * (PASSES * H + N):PACK * (PASSES * H + N) + N_TILES]
         v_w = [sb("v_w%d" % a, [P, S], U32) for a in range(PASSES)]
@@ -68,12 +68,16 @@ def tile_list_tactile_contact_torque_kernel(tc, tab_words, tab_scales, offs, wf,
         warm = sb("warm", [P, 2], F32)
         widths = [count * JB for first, count in CHUNKS]
         mag = [sb("mag%d" % q, [P, PACK, JQ], F32) for q in range(QUARTERS)]
-        root = [sb("root%d" % b, [P, PACK * JB], F32) for b in range(BLOCKS)]
+        root_pair = sb("root_pair", [P, len(ON_VECTOR), PACK * JB], F32)
+        damp_pair = sb("damp_pair", [P, len(ON_VECTOR), PACK * JB], F32, "wf_bf2")
+        root = [root_pair[:, b - ON_VECTOR[0], :] if b in ON_VECTOR else sb("root%d" % b, [P, PACK * JB], F32)[:] for b in range(BLOCKS)]
         spare = 8 * T
-        damp = [at("damp4", [P, PACK * JB], F32, spare) if b == BESIDE_CAST - 1
-                else sb("damp%d" % b, [P, PACK * JB], F32, "wf_bf2" if b == ON_VECTOR else None) for b in range(BLOCKS)]
-        wj_bf = sb("wj_bf", [P, N * PACK], BF16, "root%d" % ON_VECTOR)
-        h_bf = [sb("h_bf%d" % c, [P, w * PACK], BF16) for c, w in enumerate(widths)]
+        placed = {BESIDE_CAST - 2: spare, ON_GPSIMD: spare + 2048}
+        damp = [at("damp%d" % b, [P, PACK * JB], F32, placed[b])[:] if b in placed else damp_pair[:, b - ON_VECTOR[0], :] if b in ON_VECTOR
+                else sb("damp%d" % b, [P, PACK * JB], F32)[:] for b in range(BLOCKS)]
+        wj_bf = sb("wj_bf", [P, N * PACK], BF16, "root_pair")
+        h_bf = [at("h_bf1", [P, w * PACK], BF16, spare + 2048) if c == 1 else sb("h_bf%d" % c, [P, w * PACK], BF16, "h_bf0" if c == 2 else None)
+                for c, w in enumerate(widths)]
         h_w = [sb("h_w%d" % c, [P, w], U32) if c else at("h_w0", [P, w], U32, spare + 1024) for c, w in enumerate(widths)]
         h_s = [sb("h_s%d" % c, [P, w], U8) for c, w in enumerate(widths)]
         res = [sb("res%d" % c, [P, N_TILES, w], F32) for c, w in enumerate(widths)]
@@ -88,9 +92,6 @@ def tile_list_tactile_contact_torque_kernel(tc, tab_words, tab_scales, offs, wf,
 
         def load_table(a):
             nc.sync.dma_start(tab_w[a][:], tab_words[a].rearrange("p t i -> p (t i)").bitcast(I32))
-
-        def load_wf(a, r0, r1):
-            nc.sync.dma_start(wf_raw[a][:, :, r0:r1], wf[a * 512:(a + 1) * 512, r0:r1].rearrange("(p i) r -> p i r", i=PACK))
 
         nc.sync.dma_start(offsets[:], offs)
         ws_scales_i = ws_scales.bitcast(I32).rearrange("a q n -> (a q) n")
@@ -141,10 +142,8 @@ def tile_list_tactile_contact_torque_kernel(tc, tab_words, tab_scales, offs, wf,
         for b in range(BLOCKS):
             nc.scalar.activation(mag[b // 2][:, 2 * (b % 2):2 * (b % 2) + 2, :].rearrange("p t j -> p (t j)"), banks[b][:], ACT.Abs)
 
-        for a in range(PASSES - 1):
-            load_wf(a, 0, H)
-        for half in range(2):
-            nc.sync.dma_start(wf_last[half], wf[(PASSES - 1) * 512:, half * H // 2:(half + 1) * H // 2].rearrange("(p i) r -> p i r", i=PACK))
+        for a in range(PASSES):
+            nc.sync.dma_start(wf_raw[a], wf[a * 512:(a + 1) * 512, :].rearrange("(p i) r -> p i r", i=PACK))
         wj_rows = wj.rearrange("(g t e) n -> t g e n", t=PACK, e=4)
         for t in range(PACK):
             nc.sync.dma_start(wj_raw[:, t, :], wj_rows[t])
@@ -160,51 +159,41 @@ def tile_list_tactile_contact_torque_kernel(tc, tab_words, tab_scales, offs, wf,
             nc.vector.quantize_mx(out=wf_w[a][:, u * 256:(u + 1) * 256].bitcast(FP8X4), scales=wf_s[a][:, u * 256:(u + 1) * 256],
                                   in_=wf_bf[a][:, u * 1024:(u + 1) * 1024])
 
-        for a in range(PASSES - 1):
+        for a in range(PASSES):
             cast_wf(a, 0)
             cast_wf(a, 1)
             quant_wf(a, 0)
             quant_wf(a, 1)
-        a = PASSES - 1
-        for half in range(2):
-            for u in range(2):
-                nc.vector.tensor_copy(
-                    wf_bf[a][:].rearrange("p (t g e i) -> p t g i e", t=PACK, e=4, i=PACK)[:, 2 * u:2 * u + 2, 16 * half:16 * half + 16],
-                    wf_last[half].rearrange("p i (g t e) -> p t g i e", t=PACK, e=4)[:, 2 * u:2 * u + 2])
-            for t in range(PACK):
-                c0 = t * P + half * P // 2
-                nc.vector.quantize_mx(out=wf_w[a][:, c0:c0 + P // 2].bitcast(FP8X4), scales=wf_s[a][:, c0:c0 + P // 2],
-                                      in_=wf_bf[a][:, c0 * PACK:(c0 + P // 2) * PACK])
 
         def force(b):
             cols = slice(b * JB, (b + 1) * JB)
-            for a in range(PASSES):
+            for step, a in enumerate((0, 1, 2) if b < EARLY_BLOCKS else (0, 2, 1)):
                 for t in range(PACK):
                     nc.tensor.matmul_mx(
                         out=banks[b][:, t * JB:(t + 1) * JB], lhsT=wf_w[a][:, t * P:(t + 1) * P].bitcast(FP8X4),
                         lhsT_scale=wf_s[a][:, t * P:(t + 1) * P],
                         rhs=v_w[a][:, cols].bitcast(FP8X4), rhs_scale=planes[a][:, cols],
-                        start=(a == 0 and t == 0), stop=(a == PASSES - 1 and t == PACK - 1))
+                        start=(step == 0 and t == 0), stop=(step == PASSES - 1 and t == PACK - 1))
 
         for b in range(BESIDE_CAST):
             force(b)
 
         for b in range(BLOCKS):
-            nc.scalar.activation(root[b][:].rearrange("p (t j) -> p t j", t=PACK), mag[b // 2][:, :, (b % 2) * JB:(b % 2 + 1) * JB],
+            nc.scalar.activation(root[b].rearrange("p (t j) -> p t j", t=PACK), mag[b // 2][:, :, (b % 2) * JB:(b % 2 + 1) * JB],
                                  ACT.Abs_reciprocal_sqrt, bias=1.0)
-            if b != ON_VECTOR:
-                nc.scalar.activation(damp[b][:], root[b][:], ACT.Square)
+            if b not in ON_VECTOR and b != ON_GPSIMD:
+                nc.scalar.activation(damp[b], root[b], ACT.Square)
 
-        nc.vector.tensor_tensor(damp[ON_VECTOR][:], root[ON_VECTOR][:], root[ON_VECTOR][:], ALU.mult)
+        nc.vector.tensor_tensor(damp_pair[:], root_pair[:], root_pair[:], ALU.mult)
         nc.gpsimd.tensor_scalar(wj_bf[:].rearrange("p (n t) -> p n t", t=PACK), wj_raw.rearrange("p t n -> p n t"),
                                 1.0, 0.0, ALU.mult, ALU.add)
 
         def multiply(b):
-            c = max(i for i, (first, count) in enumerate(CHUNKS) if first <= b)
+            c = max(i for i, (first, count) in enumerate(CHUNKS) if first <= b < first + count)
             o = (b - CHUNKS[c][0]) * PACK * JB
             nc.vector.tensor_tensor(h_bf[c][:, o:o + PACK * JB].rearrange("p (c e t) -> p c t e", e=2, t=PACK),
                                     banks[b][:].rearrange("p (t c e) -> p c t e", e=2, t=PACK),
-                                    damp[b][:].rearrange("p (t c e) -> p c t e", e=2, t=PACK), ALU.mult)
+                                    damp[b].rearrange("p (t c e) -> p c t e", e=2, t=PACK), ALU.mult)
 
         def quant_h(c):
             nc.vector.quantize_mx(out=h_w[c][:].bitcast(FP8X4), scales=h_s[c][:], in_=h_bf[c][:])
@@ -216,6 +205,8 @@ def tile_list_tactile_contact_torque_kernel(tc, tab_words, tab_scales, offs, wf,
             w = widths[c]
             if count == 2:
                 return banks[first + n // 2][:, (n % 2) * w:(n % 2 + 1) * w]
+            if c == last and n == 2:
+                return banks[1][:, 0:w]
             return banks[first][:, n * w:(n + 1) * w]
 
         def finish(c):
@@ -224,7 +215,7 @@ def tile_list_tactile_contact_torque_kernel(tc, tab_words, tab_scales, offs, wf,
                 nc.tensor.matmul_mx(out=place(c, n), lhsT=wj_w[:, n * P:(n + 1) * P].bitcast(FP8X4), lhsT_scale=wj_s[:, n * P:(n + 1) * P],
                                     rhs=h_w[c][:].bitcast(FP8X4), rhs_scale=h_s[c][:], start=True, stop=True)
             for n in range(N_TILES):
-                if c >= last - 1:
+                if c == last - 1 or (c == last and n == 2):
                     nc.vector.tensor_scalar(res[c][:, n, :], place(c, n), bias[:, n:n + 1], None, ALU.add)
                 else:
                     nc.scalar.activation(res[c][:, n, :], place(c, n), ACT.Identity, bias=bias[:, n:n + 1])
@@ -237,16 +228,21 @@ def tile_list_tactile_contact_torque_kernel(tc, tab_words, tab_scales, offs, wf,
             multiply(b)
         quant_h(0)
         nc.vector.quantize_mx(out=wj_w[:].bitcast(FP8X4), scales=wj_s[:], in_=wj_bf[:])
-        finish(0)
+        force(4)
         force(5)
-        for c, (first, count) in list(enumerate(CHUNKS))[1:]:
-            for b in range(max(first, BESIDE_CAST), first + count):
-                multiply(b)
-            quant_h(c)
-            if c == last:
-                finish(c - 1)
-            if c != last - 1:
-                finish(c)
-            if c == 1:
-                force(6)
-                force(7)
+        finish(0)
+        quant_h(1)
+        nc.gpsimd.tensor_tensor(damp[ON_GPSIMD], root[ON_GPSIMD], root[ON_GPSIMD], ALU.mult)
+        finish(1)
+        force(6)
+        multiply(4)
+        force(7)
+        multiply(5)
+        multiply(7)
+        quant_h(2)
+        multiply(6)
+        quant_h(3)
+        quant_h(4)
+        finish(2)
+        finish(3)
+        finish(4)

@@ -48,13 +48,14 @@ def tile_list_tactile_contact_torque_kernel(tc, tab_words, tab_scales, offs, wf,
 
         offsets = keep.tile([P, S // 16], U16, name="offsets")
         ws_w_raw = sb("ws_w_raw", [P, PASSES, H // 2], I32)
-        planes = [sb("plane%d" % a, [P, S + H], U8) for a in range(PASSES)]
-        ws_s_raw = sb("ws_s_raw", [P, H // 4], I32)
-        tab_s = sb("tab_s", [P, T // 4], I32)
-        picked_s = at("picked_s", [P, S], U8, 4 * T - S // 2)
+        planes = [sb("plane%d" % a, [P, S], U8) for a in range(PASSES)]
+        ws_s_raw = sb("ws_s_raw", [P, PASSES, 4, H // 4], I32)
+        ws_s_dealt = sb("ws_s_dealt", [P, PASSES, 4, H // 4], I32)
+        ws_s = sb("ws_s", [P, PASSES, H], U8)
+        tab_s = at("tab_s", [P, T // 4], I32, 4 * T - T // 2)
+        picked_s = sb("picked_s", [P, S], U8)
         ws_w = sb("ws_w", [P, PASSES, H // 2], I32)
         tab_w = [sb("tab_w0", [P, T], I32, "tab0"), at("tab_w1", [P, T], I32, 0), at("tab_w2", [P, T], I32, 4 * T)]
-        staged = sb("staged", [P, (S + H) // 4], I32)
         late = sb("late", [P, PACK * (PASSES * H + N) + N_TILES], F32, "tab0")
         wf_raw = [late[:, a * PACK * H:(a + 1) * PACK * H].rearrange("p (i r) -> p i r", i=PACK) for a in range(PASSES)]
         wj_raw = late[:, PACK * PASSES * H:PACK * (PASSES * H + N)].rearrange("p (t n) -> p t n", t=PACK)
@@ -85,8 +86,7 @@ def tile_list_tactile_contact_torque_kernel(tc, tab_words, tab_scales, offs, wf,
 
         nc.vector.memset(tab_s[0:ROW0, :], 0)
         nc.gpsimd.memset(tab_s[ROW0 + ROWS:P, :], 0)
-        nc.vector.memset(ws_s_raw[0:ROW0, :], 0)
-        nc.vector.memset(ws_s_raw[ROW0 + ROWS:P, :], 0)
+        nc.vector.memset(ws_s[:].rearrange("p a n -> p (a n)").bitcast(I32), 0)
         for plane in planes:
             nc.vector.memset(plane[:].bitcast(I32), 0)
 
@@ -94,31 +94,34 @@ def tile_list_tactile_contact_torque_kernel(tc, tab_words, tab_scales, offs, wf,
             nc.sync.dma_start(tab_w[a][:], tab_words[a].rearrange("p t i -> p (t i)").bitcast(I32))
 
         nc.sync.dma_start(offsets[:], offs)
-        ws_scales_i = ws_scales.bitcast(I32).rearrange("a q n -> (a q) n")
+        ws_scales_i = ws_scales.bitcast(I32).rearrange("a (q r) n -> r (a q) n", r=4)
         tab_scales_i = tab_scales.bitcast(I32).rearrange("a q n -> (a q) n")
-        for rows_sb, rows_hbm in ((tab_s, tab_scales_i), (ws_s_raw, ws_scales_i)):
-            nc.sync.dma_start(rows_sb[ROW0:ROW0 + 32, :], rows_hbm[0:32, :])
-            nc.sync.dma_start(rows_sb[ROW0 + 32:ROW0 + ROWS, :], rows_hbm[32:ROWS, :])
+        nc.sync.dma_start(tab_s[ROW0:ROW0 + 32, :], tab_scales_i[0:32, :])
+        nc.sync.dma_start(tab_s[ROW0 + 32:ROW0 + ROWS, :], tab_scales_i[32:ROWS, :])
+        nc.sync.dma_start(ws_s_raw[0:4].rearrange("r a q n -> r (a q) n"), ws_scales_i)
         nc.sync.dma_start(ws_w_raw[:], ws_words.bitcast(I32).rearrange("a p n -> p a n"))
         load_table(0)
         nc.vector.memset(warm[:, 0:1], 1.0)
         nc.scalar.activation(warm[:, 1:2], warm[:, 0:1], ACT.Abs_reciprocal_sqrt)
 
         nc.vector.tensor_copy(picked_s[:], tab_s[:].bitcast(U8).indirect(offsets[:]))
-        nc.vector.tensor_copy(staged[:, S // 4:].rearrange("p (t g) -> p t g", t=PACK),
-                              ws_s_raw[:].rearrange("p (g t) -> p t g", t=PACK))
-        nc.vector.tensor_copy(staged[:, 0:S // 4], picked_s[:].bitcast(I32))
         for a in range(PASSES):
             if a == PASSES - 1:
                 load_table(a)
             for r in range(4):
                 row = ROW0 + 16 * a
-                nc.sync.dma_start(planes[a][r:P:32, :].bitcast(I32), staged[row + r:row + 16:4, :])
+                nc.sync.dma_start(planes[a][r:P:32, :].bitcast(I32), picked_s[row + r:row + 16:4, :].bitcast(I32))
             if a == 0:
                 load_table(1)
 
         nc.vector.tensor_copy(ws_w[:].rearrange("p a (t g w) -> p a t g w", t=PACK, w=2),
                               ws_w_raw[:].rearrange("p a (g t w) -> p a t g w", t=PACK, w=2))
+
+        ws_s_i = ws_s[:].rearrange("p a n -> p (a n)").bitcast(I32).rearrange("p (a n) -> p a n", a=PASSES)
+        nc.vector.tensor_copy(ws_s_dealt[0:4].rearrange("p a q (t g) -> p (a q) g t", t=PACK),
+                              ws_s_raw[0:4].rearrange("p a q (g t) -> p (a q) g t", t=PACK))
+        for q in range(4):
+            nc.vector.tensor_copy(ws_s_i[32 * q:32 * q + 4], ws_s_dealt[0:4, :, q, :])
 
         def gather_words(a, j0, j1):
             nc.vector.tensor_copy(v_w[a][:, j0:j1], tab_w[a][:].bitcast(U32).indirect(offsets[:, j0 // 16:j1 // 16]))
@@ -128,7 +131,7 @@ def tile_list_tactile_contact_torque_kernel(tc, tab_words, tab_scales, offs, wf,
             for t in range(PACK):
                 nc.tensor.matmul_mx(
                     out=banks[2 * q + t // 2][:, (t % 2) * JQ:(t % 2 + 1) * JQ], lhsT=ws_w[:, a, t * 64:(t + 1) * 64].bitcast(FP4X4),
-                    lhsT_scale=planes[a][:, S + t * P:S + (t + 1) * P],
+                    lhsT_scale=ws_s[:, a, t * P:(t + 1) * P],
                     rhs=v_w[a][:, cols].bitcast(FP8X4), rhs_scale=planes[a][:, cols],
                     start=(a == 0 and t % 2 == 0), stop=(a == PASSES - 1 and t % 2 == 1))
 

@@ -41,10 +41,10 @@ def tile_list_tactile_contact_torque_kernel(tc, tab_words, tab_scales, offs, wf,
         psum = ctx.enter_context(tc.psum_pool(name="psum", bufs=1))
 
         def sb(name, shape, dtype, slot=None):
-            return keep.tile(shape, dtype, name=name, tag=slot or name, align_bytes=64)
+            return keep.tile(shape, dtype, name=name, tag=slot or name, align_bytes=256)
 
         def at(name, shape, dtype, offset):
-            return laid.tile(shape, dtype, name=name, align_bytes=64, offset=offset)
+            return laid.tile(shape, dtype, name=name, align_bytes=256, offset=offset)
 
         offsets = keep.tile([P, S // 16], U16, name="offsets")
         ws_w_raw = sb("ws_w_raw", [P, PASSES, H // 2], I32)

@@ -30,7 +30,8 @@ ROW0 = 48
 ON_VECTOR = (1,)
 BESIDE_CAST = 4
 ON_GPSIMD = 6
-EARLY_BLOCKS = 5
+EARLY_BLOCKS = 4
+LATE_BANK = 4
 
 
 def tile_list_tactile_contact_torque_kernel(tc, tab_words, tab_scales, offs, wf, ws_words, ws_scales, wj, bj, out):
@@ -168,12 +169,14 @@ def tile_list_tactile_contact_torque_kernel(tc, tab_words, tab_scales, offs, wf,
             quant_wf(a, 0)
             quant_wf(a, 1)
 
+        sums = [banks[LATE_BANK if b == ON_GPSIMD else b] for b in range(BLOCKS)]
+
         def force(b):
             cols = slice(b * JB, (b + 1) * JB)
             for step, a in enumerate((0, 1, 2) if b < EARLY_BLOCKS else (0, 2, 1)):
                 for t in range(PACK):
                     nc.tensor.matmul_mx(
-                        out=banks[b][:, t * JB:(t + 1) * JB], lhsT=wf_w[a][:, t * P:(t + 1) * P].bitcast(FP8X4),
+                        out=sums[b][:, t * JB:(t + 1) * JB], lhsT=wf_w[a][:, t * P:(t + 1) * P].bitcast(FP8X4),
                         lhsT_scale=wf_s[a][:, t * P:(t + 1) * P],
                         rhs=v_w[a][:, cols].bitcast(FP8X4), rhs_scale=planes[a][:, cols],
                         start=(step == 0 and t == 0), stop=(step == PASSES - 1 and t == PACK - 1))
@@ -184,8 +187,10 @@ def tile_list_tactile_contact_torque_kernel(tc, tab_words, tab_scales, offs, wf,
         for b in range(BLOCKS):
             nc.scalar.activation(root[b].rearrange("p (t j) -> p t j", t=PACK), mag[b // 2][:, :, (b % 2) * JB:(b % 2 + 1) * JB],
                                  ACT.Abs_reciprocal_sqrt, bias=1.0)
-            if b not in ON_VECTOR and b != ON_GPSIMD:
-                nc.scalar.activation(damp[b], root[b], ACT.Square)
+            if 0 < b < ON_GPSIMD and b - 1 not in ON_VECTOR:
+                nc.scalar.activation(damp[b - 1], root[b - 1], ACT.Square)
+        for b in (ON_GPSIMD - 1, BLOCKS - 1):
+            nc.scalar.activation(damp[b], root[b], ACT.Square)
 
         nc.vector.tensor_tensor(damp_pair[:], root_pair[:], root_pair[:], ALU.mult)
         nc.gpsimd.tensor_scalar(wj_bf[:].rearrange("p (n t) -> p n t", t=PACK), wj_raw.rearrange("p t n -> p n t"),
@@ -195,7 +200,7 @@ def tile_list_tactile_contact_torque_kernel(tc, tab_words, tab_scales, offs, wf,
             c = max(i for i, (first, count) in enumerate(CHUNKS) if first <= b < first + count)
             o = (b - CHUNKS[c][0]) * PACK * JB
             nc.vector.tensor_tensor(h_bf[c][:, o:o + PACK * JB].rearrange("p (c e t) -> p c t e", e=2, t=PACK),
-                                    banks[b][:].rearrange("p (t c e) -> p c t e", e=2, t=PACK),
+                                    sums[b][:].rearrange("p (t c e) -> p c t e", e=2, t=PACK),
                                     damp[b].rearrange("p (t c e) -> p c t e", e=2, t=PACK), ALU.mult)
 
         def quant_h(c):
@@ -207,10 +212,10 @@ def tile_list_tactile_contact_torque_kernel(tc, tab_words, tab_scales, offs, wf,
             first, count = CHUNKS[c]
             w = widths[c]
             if count == 2:
-                return banks[first + n // 2][:, (n % 2) * w:(n % 2 + 1) * w]
+                return banks[ON_GPSIMD if first + n // 2 == LATE_BANK else first + n // 2][:, (n % 2) * w:(n % 2 + 1) * w]
             if c == last and n == 2:
                 return banks[1][:, 0:w]
-            return banks[first][:, n * w:(n + 1) * w]
+            return sums[first][:, n * w:(n + 1) * w]
 
         def finish(c):
             j0 = CHUNKS[c][0] * JB
@@ -237,9 +242,9 @@ def tile_list_tactile_contact_torque_kernel(tc, tab_words, tab_scales, offs, wf,
         quant_h(1)
         nc.gpsimd.tensor_tensor(damp[ON_GPSIMD], root[ON_GPSIMD], root[ON_GPSIMD], ALU.mult)
         finish(1)
-        force(6)
-        multiply(4)
         force(7)
+        multiply(4)
+        force(6)
         multiply(5)
         multiply(7)
         quant_h(2)

@@ -82,7 +82,9 @@ def tile_list_tactile_contact_torque_kernel(tc, tab_words, tab_scales, offs, wf,
                 for c, w in enumerate(widths)]
         h_w = [sb("h_w%d" % c, [P, w], U32) if c else at("h_w0", [P, w], U32, spare + 1024) for c, w in enumerate(widths)]
         h_s = [sb("h_s%d" % c, [P, w], U8) for c, w in enumerate(widths)]
-        res = [sb("res%d" % c, [P, N_TILES, w], F32) for c, w in enumerate(widths)]
+        res_end = sb("res_end", [P, N_TILES, JQ], F32)
+        res = [sb("res%d" % c, [P, N_TILES, widths[c]], F32)[:] if count == 2 else res_end[:, :, (first % 2) * JB:(first % 2 + 1) * JB]
+               for c, (first, count) in enumerate(CHUNKS)]
         banks = [psum.tile([P, PACK * JB], F32, name="bank%d" % b) for b in range(BLOCKS)]
 
         nc.vector.memset(tab_s[0:ROW0, :], 0)
@@ -227,10 +229,10 @@ def tile_list_tactile_contact_torque_kernel(tc, tab_words, tab_scales, offs, wf,
                     nc.vector.tensor_scalar(res[c][:, n, :], place(c, n), bias[:, n:n + 1], None, ALU.add)
                 else:
                     nc.scalar.activation(res[c][:, n, :], place(c, n), ACT.Identity, bias=bias[:, n:n + 1])
-                if c < 3:
+                if c < last - 1:
                     nc.sync.dma_start(out[n * P:(n + 1) * P, j0:j0 + widths[c]], res[c][:, n, :])
-            if c >= 3:
-                nc.sync.dma_start(out.rearrange("(n p) j -> p n j", p=P)[:, :, j0:j0 + widths[c]], res[c][:])
+                elif c == last:
+                    nc.sync.dma_start(out[n * P:(n + 1) * P, S - JQ:S], res_end[:, n, :])
 
         for b in range(BESIDE_CAST):
             multiply(b)

from contextlib import ExitStack

import concourse.mybir as mybir

K, T, S, H, N = 1536, 4096, 1024, 512, 384
FLOPS = 2 * S * (2 * K * H + H * N)

F32 = mybir.dt.float32
BF16 = mybir.dt.bfloat16
I32 = mybir.dt.int32
U32 = mybir.dt.uint32
U16 = mybir.dt.uint16
U8 = mybir.dt.uint8
FP8X4 = mybir.dt.float8_e4m3fn_x4
FP4X4 = mybir.dt.float4_e2m1fn_x4
ACT = mybir.ActivationFunctionType
ALU = mybir.AluOpType

P = 128
PACK = 4
PASSES = K // (P * PACK)
BLOCKS = 8
JB = S // BLOCKS
JQ = 2 * JB
QUARTERS = S // JQ
CHUNKS = ((0, 2), (2, 2), (4, 2), (7, 1), (6, 1))
N_TILES = N // P
ROWS = 16 * PASSES
ROW0 = 48
ON_VECTOR = (1,)
BESIDE_CAST = 4
ON_GPSIMD = 6
EARLY_BLOCKS = 4
LATE_BANK = 4


def tile_list_tactile_contact_torque_kernel(tc, tab_words, tab_scales, offs, wf, ws_words, ws_scales, wj, bj, out):
    nc = tc.nc
    with ExitStack() as ctx:
        keep = ctx.enter_context(tc.tile_pool(name="keep", bufs=1))
        laid = ctx.enter_context(tc.tile_pool(name="laid", bufs=1))
        psum = ctx.enter_context(tc.psum_pool(name="psum", bufs=1))

        def sb(name, shape, dtype, slot=None):
            return keep.tile(shape, dtype, name=name, tag=slot or name, align_bytes=256)

        def at(name, shape, dtype, offset):
            return laid.tile(shape, dtype, name=name, align_bytes=256, offset=offset)

        offsets = keep.tile([P, S // 16], U16, name="offsets")
        ws_w_raw = sb("ws_w_raw", [P, PASSES, H // 2], I32)
        planes = [sb("plane%d" % a, [P, S], U8) for a in range(PASSES)]
        ws_s_raw = sb("ws_s_raw", [P, PASSES, 4, H // 4], I32)
        ws_s_dealt = sb("ws_s_dealt", [P, PASSES, 4, H // 4], I32)
        ws_s = sb("ws_s", [P, PASSES, H], U8)
        tab_s = at("tab_s", [P, T // 4], I32, 4 * T - T // 2)
        picked_s = sb("picked_s", [P, S], U8)
        ws_w = sb("ws_w", [P, PASSES, H // 2], I32)
        tab_w = [sb("tab_w0", [P, T], I32, "tab0"), at("tab_w1", [P, T], I32, 0), at("tab_w2", [P, T], I32, 4 * T)]
        late = sb("late", [P, PACK * (PASSES * H + N) + N_TILES], F32, "tab0")
        wf_raw = [late[:, a * PACK * H:(a + 1) * PACK * H].rearrange("p (i r) -> p i r", i=PACK) for a in range(PASSES)]
        wj_raw = late[:, PACK * PASSES * H:PACK * (PASSES * H + N)].rearrange("p (t n) -> p t n", t=PACK)
        bias = late[:, PACK * (PASSES * H + N):PACK * (PASSES * H + N) + N_TILES]
        v_w = [sb("v_w%d" % a, [P, S], U32) for a in range(PASSES)]
        wf_bf = [sb("wf_bf%d" % a, [P, H * PACK], BF16) for a in range(PASSES)]
        wf_w = [sb("wf_w%d" % a, [P, H], U32) for a in range(PASSES)]
        wf_s = [sb("wf_s%d" % a, [P, H], U8) for a in range(PASSES)]
        wj_w = sb("wj_w", [P, N], U32)
        wj_s = sb("wj_s", [P, N], U8)
        warm = sb("warm", [P, 2], F32)
        widths = [count * JB for first, count in CHUNKS]
        mag = [sb("mag%d" % q, [P, PACK, JQ], F32) for q in range(QUARTERS)]
        root_pair = sb("root_pair", [P, len(ON_VECTOR), PACK * JB], F32)
        damp_pair = sb("damp_pair", [P, len(ON_VECTOR), PACK * JB], F32, "wf_bf2")
        root = [root_pair[:, b - ON_VECTOR[0], :] if b in ON_VECTOR else sb("root%d" % b, [P, PACK * JB], F32)[:] for b in range(BLOCKS)]
        spare = 8 * T
        placed = {BESIDE_CAST - 2: spare, ON_GPSIMD: spare + 2048}
        damp = [at("damp%d" % b, [P, PACK * JB], F32, placed[b])[:] if b in placed else damp_pair[:, b - ON_VECTOR[0], :] if b in ON_VECTOR
                else sb("damp%d" % b, [P, PACK * JB], F32)[:] for b in range(BLOCKS)]
        wj_bf = sb("wj_bf", [P, N * PACK], BF16, "root_pair")
        h_bf = [at("h_bf1", [P, w * PACK], BF16, spare + 2048) if c == 1 else sb("h_bf%d" % c, [P, w * PACK], BF16, "h_bf0" if c == 2 else None)
                for c, w in enumerate(widths)]
        h_w = [sb("h_w%d" % c, [P, w], U32) if c else at("h_w0", [P, w], U32, spare + 1024) for c, w in enumerate(widths)]
        h_s = [sb("h_s%d" % c, [P, w], U8) for c, w in enumerate(widths)]
        res_end = sb("res_end", [P, N_TILES, JQ], F32)
        res = [sb("res%d" % c, [P, N_TILES, widths[c]], F32)[:] if count == 2 else res_end[:, :, (first % 2) * JB:(first % 2 + 1) * JB]
               for c, (first, count) in enumerate(CHUNKS)]
        banks = [psum.tile([P, PACK * JB], F32, name="bank%d" % b) for b in range(BLOCKS)]

        nc.vector.memset(tab_s[0:ROW0, :], 0)
        nc.gpsimd.memset(tab_s[ROW0 + ROWS:P, :], 0)
        nc.vector.memset(ws_s[:].rearrange("p a n -> p (a n)").bitcast(I32), 0)
        for plane in planes:
            nc.vector.memset(plane[:].bitcast(I32), 0)

        def load_table(a):
            nc.sync.dma_start(tab_w[a][:], tab_words[a].rearrange("p t i -> p (t i)").bitcast(I32))

        nc.sync.dma_start(offsets[:], offs)
        ws_scales_i = ws_scales.bitcast(I32).rearrange("a (q r) n -> r (a q) n", r=4)
        tab_scales_i = tab_scales.bitcast(I32).rearrange("a q n -> (a q) n")
        nc.sync.dma_start(tab_s[ROW0:ROW0 + 32, :], tab_scales_i[0:32, :])
        nc.sync.dma_start(tab_s[ROW0 + 32:ROW0 + ROWS, :], tab_scales_i[32:ROWS, :])
        nc.sync.dma_start(ws_s_raw[0:4].rearrange("r a q n -> r (a q) n"), ws_scales_i)
        nc.sync.dma_start(ws_w_raw[:], ws_words.bitcast(I32).rearrange("a p n -> p a n"))
        load_table(0)
        nc.vector.memset(warm[:, 0:1], 1.0)
        nc.scalar.activation(warm[:, 1:2], warm[:, 0:1], ACT.Abs_reciprocal_sqrt)

        nc.vector.tensor_copy(picked_s[:], tab_s[:].bitcast(U8).indirect(offsets[:]))
        for a in range(PASSES):
            if a == PASSES - 1:
                load_table(a)
            for r in range(4):
                row = ROW0 + 16 * a
                nc.sync.dma_start(planes[a][r:P:32, :].bitcast(I32), picked_s[row + r:row + 16:4, :].bitcast(I32))
            if a == 0:
                load_table(1)

        nc.vector.tensor_copy(ws_w[:].rearrange("p a (t g w) -> p a t g w", t=PACK, w=2),
                              ws_w_raw[:].rearrange("p a (g t w) -> p a t g w", t=PACK, w=2))

        ws_s_i = ws_s[:].rearrange("p a n -> p (a n)").bitcast(I32).rearrange("p (a n) -> p a n", a=PASSES)
        nc.vector.tensor_copy(ws_s_dealt[0:4].rearrange("p a q (t g) -> p (a q) g t", t=PACK),
                              ws_s_raw[0:4].rearrange("p a q (g t) -> p (a q) g t", t=PACK))
        for q in range(4):
            nc.vector.tensor_copy(ws_s_i[32 * q:32 * q + 4], ws_s_dealt[0:4, :, q, :])

        def gather_words(a, j0, j1):
            nc.vector.tensor_copy(v_w[a][:, j0:j1], tab_w[a][:].bitcast(U32).indirect(offsets[:, j0 // 16:j1 // 16]))

        def stiff(a, q):
            cols = slice(q * JQ, (q + 1) * JQ)
            for t in range(PACK):
                nc.tensor.matmul_mx(
                    out=banks[2 * q + t // 2][:, (t % 2) * JQ:(t % 2 + 1) * JQ], lhsT=ws_w[:, a, t * 64:(t + 1) * 64].bitcast(FP4X4),
                    lhsT_scale=ws_s[:, a, t * P:(t + 1) * P],
                    rhs=v_w[a][:, cols].bitcast(FP8X4), rhs_scale=planes[a][:, cols],
                    start=(a == 0 and t % 2 == 0), stop=(a == PASSES - 1 and t % 2 == 1))

        for a in range(PASSES):
            step = 1 if a == PASSES - 1 else 2
            for q in range(0, QUARTERS, step):
                gather_words(a, q * JQ, (q + step) * JQ)
                for each in range(q, q + step):
                    stiff(a, each)

        for b in range(BLOCKS):
            nc.scalar.activation(mag[b // 2][:, 2 * (b % 2):2 * (b % 2) + 2, :].rearrange("p t j -> p (t j)"), banks[b][:], ACT.Abs)

        for a in range(PASSES):
            nc.sync.dma_start(wf_raw[a], wf[a * 512:(a + 1) * 512, :].rearrange("(p i) r -> p i r", i=PACK))
        wj_rows = wj.rearrange("(g t e) n -> t g e n", t=PACK, e=4)
        for t in range(PACK):
            nc.sync.dma_start(wj_raw[:, t, :], wj_rows[t])
        with nc.allow_non_contiguous_dma(reason="one bias value a partition"):
            nc.sync.dma_start(bias, bj.rearrange("(c p) -> p c", p=P))

        def cast_wf(a, u):
            nc.vector.tensor_copy(
                wf_bf[a][:].rearrange("p (t g e i) -> p t g i e", t=PACK, e=4, i=PACK)[:, 2 * u:2 * u + 2],
                wf_raw[a].rearrange("p i (g t e) -> p t g i e", t=PACK, e=4)[:, 2 * u:2 * u + 2])

        def quant_wf(a, u):
            nc.vector.quantize_mx(out=wf_w[a][:, u * 256:(u + 1) * 256].bitcast(FP8X4), scales=wf_s[a][:, u * 256:(u + 1) * 256],
                                  in_=wf_bf[a][:, u * 1024:(u + 1) * 1024])

        for a in range(PASSES):
            cast_wf(a, 0)
            cast_wf(a, 1)
            quant_wf(a, 0)
            quant_wf(a, 1)

        sums = [banks[LATE_BANK if b == ON_GPSIMD else b] for b in range(BLOCKS)]

        def force(b):
            cols = slice(b * JB, (b + 1) * JB)
            for step, a in enumerate((0, 1, 2) if b < EARLY_BLOCKS else (0, 2, 1)):
                for t in range(PACK):
                    nc.tensor.matmul_mx(
                        out=sums[b][:, t * JB:(t + 1) * JB], lhsT=wf_w[a][:, t * P:(t + 1) * P].bitcast(FP8X4),
                        lhsT_scale=wf_s[a][:, t * P:(t + 1) * P],
                        rhs=v_w[a][:, cols].bitcast(FP8X4), rhs_scale=planes[a][:, cols],
                        start=(step == 0 and t == 0), stop=(step == PASSES - 1 and t == PACK - 1))

        for b in range(BESIDE_CAST):
            force(b)

        for b in range(BLOCKS):
            nc.scalar.activation(root[b].rearrange("p (t j) -> p t j", t=PACK), mag[b // 2][:, :, (b % 2) * JB:(b % 2 + 1) * JB],
                                 ACT.Abs_reciprocal_sqrt, bias=1.0)
            if 0 < b < ON_GPSIMD and b - 1 not in ON_VECTOR:
                nc.scalar.activation(damp[b - 1], root[b - 1], ACT.Square)
        for b in (ON_GPSIMD - 1, BLOCKS - 1):
            nc.scalar.activation(damp[b], root[b], ACT.Square)

        nc.vector.tensor_tensor(damp_pair[:], root_pair[:], root_pair[:], ALU.mult)
        nc.gpsimd.tensor_scalar(wj_bf[:].rearrange("p (n t) -> p n t", t=PACK), wj_raw.rearrange("p t n -> p n t"),
                                1.0, 0.0, ALU.mult, ALU.add)

        def multiply(b):
            c = max(i for i, (first, count) in enumerate(CHUNKS) if first <= b < first + count)
            o = (b - CHUNKS[c][0]) * PACK * JB
            nc.vector.tensor_tensor(h_bf[c][:, o:o + PACK * JB].rearrange("p (c e t) -> p c t e", e=2, t=PACK),
                                    sums[b][:].rearrange("p (t c e) -> p c t e", e=2, t=PACK),
                                    damp[b].rearrange("p (t c e) -> p c t e", e=2, t=PACK), ALU.mult)

        def quant_h(c):
            nc.vector.quantize_mx(out=h_w[c][:].bitcast(FP8X4), scales=h_s[c][:], in_=h_bf[c][:])

        last = len(CHUNKS) - 1

        def place(c, n):
            first, count = CHUNKS[c]
            w = widths[c]
            if count == 2:
                return banks[ON_GPSIMD if first + n // 2 == LATE_BANK else first + n // 2][:, (n % 2) * w:(n % 2 + 1) * w]
            if c == last and n == 2:
                return banks[1][:, 0:w]
            return sums[first][:, n * w:(n + 1) * w]

        def finish(c):
            j0 = CHUNKS[c][0] * JB
            for n in range(N_TILES):
                nc.tensor.matmul_mx(out=place(c, n), lhsT=wj_w[:, n * P:(n + 1) * P].bitcast(FP8X4), lhsT_scale=wj_s[:, n * P:(n + 1) * P],
                                    rhs=h_w[c][:].bitcast(FP8X4), rhs_scale=h_s[c][:], start=True, stop=True)
            for n in range(N_TILES):
                if c == last - 1 or (c == last and n == 2):
                    nc.vector.tensor_scalar(res[c][:, n, :], place(c, n), bias[:, n:n + 1], None, ALU.add)
                else:
                    nc.scalar.activation(res[c][:, n, :], place(c, n), ACT.Identity, bias=bias[:, n:n + 1])
                if c < last - 1:
                    nc.sync.dma_start(out[n * P:(n + 1) * P, j0:j0 + widths[c]], res[c][:, n, :])
                elif c == last:
                    nc.sync.dma_start(out[n * P:(n + 1) * P, S - JQ:S], res_end[:, n, :])

        for b in range(BESIDE_CAST):
            multiply(b)
        quant_h(0)
        nc.vector.quantize_mx(out=wj_w[:].bitcast(FP8X4), scales=wj_s[:], in_=wj_bf[:])
        force(4)
        force(5)
        finish(0)
        quant_h(1)
        nc.gpsimd.tensor_tensor(damp[ON_GPSIMD], root[ON_GPSIMD], root[ON_GPSIMD], ALU.mult)
        finish(1)
        force(7)
        multiply(4)
        force(6)
        multiply(5)
        multiply(7)
        quant_h(2)
        multiply(6)
        quant_h(3)
        quant_h(4)
        finish(2)
        finish(3)
        finish(4)
